import numpy as np
import ml_dtypes


def mxq(x, axis, fmt="e4m3"):
    dtype, down = {"e4m3": (ml_dtypes.float8_e4m3fn, 7), "e5m2": (ml_dtypes.float8_e5m2, 14)}[fmt]
    v = np.moveaxis(np.asarray(x, np.float32).astype(ml_dtypes.bfloat16).astype(np.float64), axis, -1)
    blocks = v.reshape(v.shape[:-1] + (-1, 32))
    amax = np.abs(blocks).max(-1, keepdims=True)
    byte = np.maximum(np.where(amax > 0, np.frexp(amax)[1] - 1 + 127, 0) - down, 1)
    scale = np.exp2(byte - 127.0)
    codes = (blocks / scale).astype(np.float32).astype(dtype).astype(np.float64)
    return np.moveaxis((codes * scale).reshape(v.shape), -1, axis)


WIDE = False


def mx_kscale(k):
    if not WIDE:
        return np.ones(k)
    levels = np.array([10, -10, 5, -5, 0])
    if k % 512:
        return np.exp2(np.random.permutation(np.resize(levels, k // 32))).repeat(32)
    a = np.empty((k // 512, 16))
    for p in range(k // 512):
        a[p, :8] = np.random.permutation(np.resize(levels, 8))
        for g in range(8):
            far = levels[np.abs(levels - a[p, g]) >= 10]
            a[p, g + 8] = far[np.random.randint(len(far))]
    return np.exp2(a.ravel()).repeat(32)


def f64(x):
    return np.asarray(x).astype(np.float64)


def striped(idx):
    return np.tile(idx.reshape(-1, 16).T, (8, 1)).astype(np.uint16)


def unstriped(offs):
    return offs[:16].T.reshape(-1).astype(np.int64)


E2M1 = np.array([0.0, 0.5, 1.0, 1.5, 2.0, 3.0, 4.0, 6.0, -0.0, -0.5, -1.0, -1.5, -2.0, -3.0, -4.0, -6.0])


def pack_weight(w, fmt):
    k, n = w.shape
    w = f64(np.asarray(w, np.float32).astype(ml_dtypes.bfloat16)).reshape(k // 32, 32, n)
    amax = np.abs(w).max(1)
    if fmt == "e4m3":
        byte = np.frexp(amax)[1] - 1 + 127 - 7
    else:
        mant, ex = np.frexp(amax / 6.0)
        byte = np.where(mant > 0.5, ex, ex - 1) + 127
    byte = np.clip(np.where(amax > 0, byte, 1), 1, 254)
    scaled = (w * np.exp2(127.0 - byte)[:, None, :]).reshape(k, n).astype(np.float32)
    by_word = np.ascontiguousarray(scaled.reshape(k // 512, 128, 4, n).transpose(0, 1, 3, 2))
    if fmt == "e4m3":
        words = by_word.astype(ml_dtypes.float8_e4m3fn).view(np.uint8)
    else:
        c = by_word.astype(ml_dtypes.float4_e2m1fn).view(np.uint8) & 0xF
        words = (c[..., 0::2] | (c[..., 1::2] << 4)).reshape(k // 512, 128, 2 * n)
    return np.ascontiguousarray(words), np.ascontiguousarray(byte.astype(np.uint8).reshape(k // 512, 16, n))


def unpack_weight(words, scales, fmt):
    g, _, n = scales.shape
    words = np.ascontiguousarray(words).reshape(g, 128, n, -1)
    if fmt == "e4m3":
        vals = words.view(ml_dtypes.float8_e4m3fn).astype(np.float64)
    else:
        nib = np.empty((g, 128, n, 4), np.uint8)
        nib[..., 0::2] = words & 0xF
        nib[..., 1::2] = words >> 4
        vals = E2M1[nib]
    vals = vals * np.repeat(np.exp2(scales.astype(np.float64) - 127.0), 8, axis=1)[..., None]
    return vals.transpose(0, 1, 3, 2).reshape(g * 512, n)


def relu2(v):
    return np.maximum(v, 0.0) ** 2


K, T, E, C, N = 512, 512, 4, 128, 384
M = 512


def by_expert(wq, xq):
    return np.concatenate([wq[e].T @ xq[:, e * C:(e + 1) * C] for e in range(E)], axis=1)


def setup_inputs():
    n = np.random.standard_normal
    s = mx_kscale(K)[:, None]
    w = [pack_weight(m, "e2m1") for m in n((E, K, N)) / np.sqrt(K) / s[None]]
    r = mx_kscale(M)[:, None]
    return {
        "uT": (n((M, T)) * r).astype(np.float32),
        "wu": (n((M, K)) / np.sqrt(M) / r * s.T).astype(np.float32),
        "w_words": np.stack([m[0] for m in w]),
        "w_scales": np.stack([m[1] for m in w]),
        "b": (0.3 * n((N, E))).astype(np.float32),
        "gate": np.tile(np.random.uniform(0.2, 1.0, E * C), (N, 1)).astype(np.float32),
        "offs": striped(np.random.permutation(T)[:E * C]),
    }


def reference(uT, wu, w_words, w_scales, b, gate, offs):
    idx = unstriped(offs)
    w = np.stack([unpack_weight(w_words[e], w_scales[e], "e2m1") for e in range(E)])
    x = mxq(f64(wu), 0, "e4m3").T @ mxq(f64(uT), 0, "e4m3")
    xq = mxq(x[:, idx], 0, "e4m3")
    y = by_expert(w, xq)
    y = relu2(y + np.repeat(f64(b), C, axis=1))
    out = np.zeros((N, T))
    out[:, idx] = f64(gate) * y
    return out

@@ -1,0 +1,151 @@
+from contextlib import ExitStack
+
+import concourse.mybir as mybir
+
+F32 = mybir.dt.float32
+BF16 = mybir.dt.bfloat16
+U32 = mybir.dt.uint32
+I32 = mybir.dt.int32
+U16 = mybir.dt.uint16
+U8 = mybir.dt.uint8
+FP8X4 = mybir.dt.float8_e4m3fn_x4
+FP4X4 = mybir.dt.float4_e2m1fn_x4
+ACT = mybir.ActivationFunctionType
+ALU = mybir.AluOpType
+
+P = 128
+PACK = 4
+M, K, T, E, C, N = 512, 512, 512, 4, 128, 384
+NC = N // P
+FLOPS = 2 * M * K * T + 2 * K * N * T
+
+
+def tile_moe_prv_lin_relu2_kernel(tc, uT, wu, w_words, w_scales, b, gate, offs, out):
+    nc = tc.nc
+    with ExitStack() as ctx:
+        keep = ctx.enter_context(tc.tile_pool(name="keep", bufs=1))
+        psum = ctx.enter_context(tc.psum_pool(name="psum", bufs=1))
+
+        offsets = keep.tile([P, E * C // 16], U16, name="offsets")
+        nc.sync.dma_start(offsets[:], offs)
+
+        u_rows = uT.rearrange("(p j) t -> p j t", j=PACK)
+        u_raw = [keep.tile([P, 2, T], F32, name=f"u_raw{h}") for h in range(2)]
+        for h in range(2):
+            nc.sync.dma_start(u_raw[h][:], u_rows[:, 2 * h : 2 * h + 2, :])
+        wu_rows = wu.rearrange("(p j) k -> p j k", j=PACK)
+        wu_raw = [keep.tile([P, PACK, K // 2], F32, name=f"wu_raw{h}") for h in range(2)]
+        for h in range(2):
+            nc.sync.dma_start(wu_raw[h][:], wu_rows[:, :, h * (K // 2) : (h + 1) * (K // 2)])
+
+        w_plane = keep.tile([P, E * N], U8, name="w_plane", align_bytes=64)
+        nc.gpsimd.memset(w_plane[:].bitcast(I32), 0)
+        for q in range(4):
+            nc.sync.dma_start(
+                w_plane[32 * q : 32 * q + 4, :].bitcast(I32).rearrange("r (e n) -> r e n", e=E),
+                w_scales[:, 0, 4 * q : 4 * q + 4, :].bitcast(I32).rearrange("e r n -> r e n"),
+            )
+        w_codes = keep.tile([P, E * 2 * N], U8, name="w_codes", align_bytes=64)
+        nc.sync.dma_start(
+            w_codes[:].bitcast(I32).rearrange("p (e n) -> p e n", e=E),
+            w_words[:, 0, :, :].bitcast(I32).rearrange("e p n -> p e n"),
+        )
+        bias = keep.tile([P, NC, E], F32, name="bias")
+        nc.sync.dma_start(bias[:], b.rearrange("(c p) e -> p c e", p=P))
+        gates = [keep.tile([P, E * C], F32, name=f"gate{c}") for c in range(NC)]
+        for c in range(NC):
+            nc.sync.dma_start(gates[c][:], gate[c * P : (c + 1) * P, :])
+
+        u_pairs = [keep.tile([P, T * 2], BF16, name=f"u_pairs{h}", align_bytes=64) for h in range(2)]
+        nc.vector.tensor_copy(u_pairs[0][:].rearrange("p (t j) -> p t j", j=2), u_raw[0][:].rearrange("p j t -> p t j"))
+        nc.scalar.copy(u_pairs[1][:].rearrange("p (t j) -> p t j", j=2), u_raw[1][:].rearrange("p j t -> p t j"))
+
+        u_codes = keep.tile([P, E * C], U32, name="u_codes", align_bytes=64)
+        u_plane = keep.tile([P, E * C], U8, name="u_plane", align_bytes=64)
+
+        def slot_offsets(e0, e1):
+            return offsets[:, e0 * (C // 16) : e1 * (C // 16)]
+
+        def gather(e0, e1):
+            u_slots = keep.tile([P, (e1 - e0) * C * PACK], BF16, name=f"u_slots{e0}", align_bytes=64)
+            words = u_slots[:].bitcast(U32).rearrange("p (s h) -> p s h", h=2)
+            for h in range(2):
+                nc.vector.tensor_copy(words[:, :, h], u_pairs[h][:].bitcast(U32).indirect(slot_offsets(e0, e1)))
+            nc.vector.quantize_mx(
+                out=u_codes[:, e0 * C : e1 * C].bitcast(FP8X4), scales=u_plane[:, e0 * C : e1 * C], in_=u_slots[:]
+            )
+
+        gather_groups = ((0, 1), (1, 2), (2, 4))
+        scatter_groups = ((0, 1), (1, 2), (2, 4))
+        gather(*gather_groups[0])
+        y = keep.tile([P, NC, E * C], F32, name="y")
+
+        wu_grouped = keep.tile([P, K * PACK], BF16, name="wu_grouped", align_bytes=64)
+        wu_dst = wu_grouped[:].rearrange("p (t m j) -> p m t j", t=PACK, j=PACK)
+        half = P // 2
+        for h, on_vector in ((0, 0), (1, 48)):
+            src = wu_raw[h][:].rearrange("p j (m t) -> p m t j", t=PACK)
+            if on_vector > 0:
+                nc.vector.tensor_copy(wu_dst[:, h * half : h * half + on_vector], src[:, :on_vector])
+            nc.scalar.copy(wu_dst[:, h * half + on_vector : (h + 1) * half], src[:, on_vector:])
+        wu_codes = keep.tile([P, K], U32, name="wu_codes", align_bytes=64)
+        wu_plane = keep.tile([P, K], U8, name="wu_plane", align_bytes=64)
+        for t in range(PACK):
+            nc.vector.quantize_mx(
+                out=wu_codes[:, t * P : (t + 1) * P].bitcast(FP8X4),
+                scales=wu_plane[:, t * P : (t + 1) * P],
+                in_=wu_grouped[:, t * P * PACK : (t + 1) * P * PACK],
+            )
+
+        def expert(e):
+            slots = slice(e * C, (e + 1) * C)
+            x_sums = psum.tile([P, PACK, C], F32, name=f"x_sums{e}")
+            for t in range(PACK):
+                nc.tensor.matmul_mx(
+                    out=x_sums[:, t, :],
+                    lhsT=wu_codes[:, t * P : (t + 1) * P].bitcast(FP8X4),
+                    lhsT_scale=wu_plane[:, t * P : (t + 1) * P],
+                    rhs=u_codes[:, slots].bitcast(FP8X4),
+                    rhs_scale=u_plane[:, slots],
+                    start=True,
+                    stop=True,
+                )
+            x_grouped = keep.tile([P, C * PACK], BF16, name=f"x_grouped{e}", align_bytes=64)
+            nc.scalar.copy(x_grouped[:].rearrange("p (s t) -> p s t", t=PACK), x_sums[:].rearrange("p t s -> p s t"))
+            x_codes = keep.tile([P, C], U32, name=f"x_codes{e}", align_bytes=64)
+            x_plane = keep.tile([P, C], U8, name=f"x_plane{e}", align_bytes=64)
+            nc.vector.quantize_mx(out=x_codes[:].bitcast(FP8X4), scales=x_plane[:], in_=x_grouped[:])
+            y_sums = psum.tile([P, NC, C], F32, name=f"y_sums{e}")
+            for c in range(NC):
+                col = e * N + c * P
+                nc.tensor.matmul_mx(
+                    out=y_sums[:, c, :],
+                    lhsT=w_codes[:, 2 * col : 2 * (col + P)].bitcast(FP4X4),
+                    lhsT_scale=w_plane[:, col : col + P],
+                    rhs=x_codes[:].bitcast(FP8X4),
+                    rhs_scale=x_plane[:],
+                    start=True,
+                    stop=True,
+                )
+            relu = keep.tile([P, NC, C], F32, name=f"relu{e}")
+            for c in range(NC):
+                nc.scalar.activation(relu[:, c, :], y_sums[:, c, :], ACT.Relu, bias=bias[:, c, e : e + 1])
+            if e == 0:
+                for c in range(NC):
+                    nc.scalar.activation(y[:, c, slots], relu[:, c, :], ACT.Square)
+            else:
+                nc.scalar.activation(y[:, :, slots], relu[:], ACT.Square)
+
+        for e0, e1 in gather_groups:
+            if e0 > 0:
+                gather(e0, e1)
+            for e in range(e0, e1):
+                expert(e)
+
+        outs = [keep.tile([P, T], F32, name=f"out{c}") for c in range(NC)]
+        for e0, e1 in scatter_groups:
+            slots = slice(e0 * C, e1 * C)
+            for c in range(NC):
+                nc.vector.tensor_tensor(outs[c][:].indirect(slot_offsets(e0, e1)), y[:, c, slots], gates[c][:, slots], ALU.mult)
+        for c in range(NC):
+            nc.sync.dma_start(out[c * P : (c + 1) * P, :], outs[c][:])

@@ -27,17 +27,22 @@ def tile_moe_prv_lin_relu2_kernel(tc, uT, wu, w_words, w_scales, b, gate, offs, 
         psum = ctx.enter_context(tc.psum_pool(name="psum", bufs=1))
 
         offsets = keep.tile([P, E * C // 16], U16, name="offsets")
-        nc.sync.dma_start(offsets[:], offs)
-
         u_rows = uT.rearrange("(p j) t -> p j t", j=PACK)
         u_raw = [keep.tile([P, 2, T], F32, name=f"u_raw{h}") for h in range(2)]
-        for h in range(2):
-            nc.sync.dma_start(u_raw[h][:], u_rows[:, 2 * h : 2 * h + 2, :])
         wu_rows = wu.rearrange("(p j) k -> p j k", j=PACK)
-        wu_raw = [keep.tile([P, PACK, K // 2], F32, name=f"wu_raw{h}") for h in range(2)]
+        wu_raw = [keep.tile([P, PACK, K // 2], F32, name=f"wu_raw{h}", tag=f"wu_raw{h}", align_bytes=64) for h in range(2)]
+        nc.sync.dma_start(u_raw[0][:], u_rows[:, 0:2, :])
+        nc.sync.dma_start(offsets[:], offs)
+        nc.sync.dma_start(u_raw[1][:], u_rows[:, 2:4, :])
         for h in range(2):
             nc.sync.dma_start(wu_raw[h][:], wu_rows[:, :, h * (K // 2) : (h + 1) * (K // 2)])
-
+        bias = keep.tile([P, NC, E], F32, name="bias")
+        nc.sync.dma_start(bias[:], b.rearrange("(c p) e -> p c e", p=P))
+        w_codes = keep.tile([P, E * 2 * N], U8, name="w_codes", align_bytes=64)
+        nc.sync.dma_start(
+            w_codes[:].bitcast(I32).rearrange("p (e n) -> p e n", e=E),
+            w_words[:, 0, :, :].bitcast(I32).rearrange("e p n -> p e n"),
+        )
         w_plane = keep.tile([P, E * N], U8, name="w_plane", align_bytes=64)
         nc.gpsimd.memset(w_plane[:].bitcast(I32), 0)
         for q in range(4):
@@ -45,107 +50,143 @@ def tile_moe_prv_lin_relu2_kernel(tc, uT, wu, w_words, w_scales, b, gate, offs, 
                 w_plane[32 * q : 32 * q + 4, :].bitcast(I32).rearrange("r (e n) -> r e n", e=E),
                 w_scales[:, 0, 4 * q : 4 * q + 4, :].bitcast(I32).rearrange("e r n -> r e n"),
             )
-        w_codes = keep.tile([P, E * 2 * N], U8, name="w_codes", align_bytes=64)
-        nc.sync.dma_start(
-            w_codes[:].bitcast(I32).rearrange("p (e n) -> p e n", e=E),
-            w_words[:, 0, :, :].bitcast(I32).rearrange("e p n -> p e n"),
-        )
-        bias = keep.tile([P, NC, E], F32, name="bias")
-        nc.sync.dma_start(bias[:], b.rearrange("(c p) e -> p c e", p=P))
-        gates = [keep.tile([P, E * C], F32, name=f"gate{c}") for c in range(NC)]
-        for c in range(NC):
-            nc.sync.dma_start(gates[c][:], gate[c * P : (c + 1) * P, :])
+        gates = keep.tile([P, NC, E * C], F32, name="gates")
+        nc.sync.dma_start(gates[:], gate.rearrange("(c p) s -> p c s", p=P))
 
         u_pairs = [keep.tile([P, T * 2], BF16, name=f"u_pairs{h}", align_bytes=64) for h in range(2)]
-        nc.vector.tensor_copy(u_pairs[0][:].rearrange("p (t j) -> p t j", j=2), u_raw[0][:].rearrange("p j t -> p t j"))
-        nc.scalar.copy(u_pairs[1][:].rearrange("p (t j) -> p t j", j=2), u_raw[1][:].rearrange("p j t -> p t j"))
-
-        u_codes = keep.tile([P, E * C], U32, name="u_codes", align_bytes=64)
-        u_plane = keep.tile([P, E * C], U8, name="u_plane", align_bytes=64)
+        pairs_dst = [u_pairs[h][:].rearrange("p (t j) -> p t j", j=2) for h in range(2)]
+        pairs_src = [u_raw[h][:].rearrange("p j t -> p t j") for h in range(2)]
+        nc.vector.tensor_copy(pairs_dst[0][:, :336], pairs_src[0][:, :336])
+        nc.scalar.copy(pairs_dst[0][:, 336:], pairs_src[0][:, 336:])
+        nc.scalar.copy(pairs_dst[1], pairs_src[1])
 
         def slot_offsets(e0, e1):
             return offsets[:, e0 * (C // 16) : e1 * (C // 16)]
 
-        def gather(e0, e1):
-            u_slots = keep.tile([P, (e1 - e0) * C * PACK], BF16, name=f"u_slots{e0}", align_bytes=64)
+        u_quantised = {}
+
+        def quantise_u(e0, e1, u_slots, plane_tag):
+            u_codes = keep.tile([P, (e1 - e0) * C], U32, name=f"u_codes{e0}", align_bytes=64)
+            u_plane = keep.tile([P, (e1 - e0) * C], U8, name=f"u_plane{e0}", tag=plane_tag, align_bytes=64)
+            nc.vector.quantize_mx(out=u_codes[:].bitcast(FP8X4), scales=u_plane[:], in_=u_slots[:])
+            for e in range(e0, e1):
+                cols = slice((e - e0) * C, (e - e0 + 1) * C)
+                u_quantised[e] = (u_codes[:, cols], u_plane[:, cols])
+
+        def gather(e):
+            u_slots = keep.tile([P, C * PACK], BF16, name=f"u_slots{e}", align_bytes=64)
             words = u_slots[:].bitcast(U32).rearrange("p (s h) -> p s h", h=2)
             for h in range(2):
-                nc.vector.tensor_copy(words[:, :, h], u_pairs[h][:].bitcast(U32).indirect(slot_offsets(e0, e1)))
-            nc.vector.quantize_mx(
-                out=u_codes[:, e0 * C : e1 * C].bitcast(FP8X4), scales=u_plane[:, e0 * C : e1 * C], in_=u_slots[:]
-            )
+                nc.vector.tensor_copy(words[:, :, h], u_pairs[h][:].bitcast(U32).indirect(slot_offsets(e, e + 1)))
+            quantise_u(e, e + 1, u_slots, ("up0", "wu_raw1")[e])
 
-        gather_groups = ((0, 1), (1, 2), (2, 4))
-        scatter_groups = ((0, 1), (1, 2), (2, 4))
-        gather(*gather_groups[0])
-        y = keep.tile([P, NC, E * C], F32, name="y")
+        gather(0)
 
-        wu_grouped = keep.tile([P, K * PACK], BF16, name="wu_grouped", align_bytes=64)
-        wu_dst = wu_grouped[:].rearrange("p (t m j) -> p m t j", t=PACK, j=PACK)
+        block = P * PACK
+        stage = keep.tile([P, (PACK + 1) * block], BF16, name="stage", align_bytes=64)
+        wu_grouped = stage[:, block:]
+        wu_dst = wu_grouped.rearrange("p (t m j) -> p m t j", t=PACK, j=PACK)
         half = P // 2
-        for h, on_vector in ((0, 0), (1, 48)):
-            src = wu_raw[h][:].rearrange("p j (m t) -> p m t j", t=PACK)
-            if on_vector > 0:
-                nc.vector.tensor_copy(wu_dst[:, h * half : h * half + on_vector], src[:, :on_vector])
-            nc.scalar.copy(wu_dst[:, h * half + on_vector : (h + 1) * half], src[:, on_vector:])
+        wu_src = [wu_raw[h][:].rearrange("p j (m t) -> p m t j", t=PACK) for h in range(2)]
+        nc.scalar.copy(wu_dst[:, :half], wu_src[0])
+        nc.vector.tensor_copy(wu_dst[:, half : half + 56], wu_src[1][:, :56])
+        nc.scalar.copy(wu_dst[:, half + 56 :], wu_src[1][:, 56:])
         wu_codes = keep.tile([P, K], U32, name="wu_codes", align_bytes=64)
         wu_plane = keep.tile([P, K], U8, name="wu_plane", align_bytes=64)
         for t in range(PACK):
             nc.vector.quantize_mx(
                 out=wu_codes[:, t * P : (t + 1) * P].bitcast(FP8X4),
                 scales=wu_plane[:, t * P : (t + 1) * P],
-                in_=wu_grouped[:, t * P * PACK : (t + 1) * P * PACK],
+                in_=wu_grouped[:, t * block : (t + 1) * block],
             )
 
-        def expert(e):
-            slots = slice(e * C, (e + 1) * C)
-            x_sums = psum.tile([P, PACK, C], F32, name=f"x_sums{e}")
-            for t in range(PACK):
-                nc.tensor.matmul_mx(
-                    out=x_sums[:, t, :],
-                    lhsT=wu_codes[:, t * P : (t + 1) * P].bitcast(FP8X4),
-                    lhsT_scale=wu_plane[:, t * P : (t + 1) * P],
-                    rhs=u_codes[:, slots].bitcast(FP8X4),
-                    rhs_scale=u_plane[:, slots],
-                    start=True,
-                    stop=True,
-                )
-            x_grouped = keep.tile([P, C * PACK], BF16, name=f"x_grouped{e}", align_bytes=64)
-            nc.scalar.copy(x_grouped[:].rearrange("p (s t) -> p s t", t=PACK), x_sums[:].rearrange("p t s -> p s t"))
-            x_codes = keep.tile([P, C], U32, name=f"x_codes{e}", align_bytes=64)
-            x_plane = keep.tile([P, C], U8, name=f"x_plane{e}", align_bytes=64)
+        def gather_late():
+            for h in range(2):
+                row = stage[:, h * PACK * block : (h * PACK + 1) * block]
+                nc.vector.tensor_copy(row.bitcast(U32), u_pairs[h][:].bitcast(U32).indirect(slot_offsets(2, E)))
+            u_slots = keep.tile([P, 2 * C * PACK], BF16, name="u_slots2", align_bytes=64)
+            rows = stage[:].bitcast(I32).rearrange("p (r s) -> p s r", r=PACK + 1)
+            nc.vector.tensor_copy(u_slots[:].bitcast(I32).rearrange("p (s h) -> p s h", h=2), rows[:, :, ::PACK])
+            quantise_u(2, E, u_slots, "xp0")
+
+        x_quantised = {}
+        y_sums = {}
+        y = {}
+        outs = [keep.tile([P, T], F32, name=f"out{c}") for c in range(NC)]
+
+        def front(e0, e1):
+            x_grouped = keep.tile([P, (e1 - e0) * C * PACK], BF16, name=f"x_grouped{e0}", align_bytes=64)
+            for e in range(e0, e1):
+                u_codes, u_plane = u_quantised[e]
+                x_sums = psum.tile([P, PACK, C], F32, name=f"x_sums{e}", tag=f"xs{e}")
+                for t in range(PACK):
+                    nc.tensor.matmul_mx(
+                        out=x_sums[:, t, :],
+                        lhsT=wu_codes[:, t * P : (t + 1) * P].bitcast(FP8X4),
+                        lhsT_scale=wu_plane[:, t * P : (t + 1) * P],
+                        rhs=u_codes.bitcast(FP8X4),
+                        rhs_scale=u_plane,
+                        start=True,
+                        stop=True,
+                    )
+                part = x_grouped[:, (e - e0) * C * PACK : (e - e0 + 1) * C * PACK]
+                nc.scalar.copy(part.rearrange("p (s t) -> p s t", t=PACK), x_sums[:].rearrange("p t s -> p s t"))
+            x_codes = keep.tile([P, (e1 - e0) * C], U32, name=f"x_codes{e0}", tag=("xc0", "xc1", "y01")[e0], align_bytes=64)
+            x_plane = keep.tile([P, (e1 - e0) * C], U8, name=f"x_plane{e0}", tag=f"xp{e0}", align_bytes=64)
             nc.vector.quantize_mx(out=x_codes[:].bitcast(FP8X4), scales=x_plane[:], in_=x_grouped[:])
-            y_sums = psum.tile([P, NC, C], F32, name=f"y_sums{e}")
+            for e in range(e0, e1):
+                cols = slice((e - e0) * C, (e - e0 + 1) * C)
+                x_quantised[e] = (x_codes[:, cols], x_plane[:, cols])
+
+        def middle(e):
+            x_codes, x_plane = x_quantised[e]
+            bank = psum.tile([P, NC, C], F32, name=f"y_sums{e}", tag=("ys0", "ys1", "ys2", "xs0")[e])
+            y_sums[e] = [bank[:, c, :] for c in range(NC)]
+            if e == 0:
+                first_bank = psum.tile([P, C], F32, name="y_first")
+                y_sums[e][0] = first_bank[:]
             for c in range(NC):
                 col = e * N + c * P
                 nc.tensor.matmul_mx(
-                    out=y_sums[:, c, :],
+                    out=y_sums[e][c],
                     lhsT=w_codes[:, 2 * col : 2 * (col + P)].bitcast(FP4X4),
                     lhsT_scale=w_plane[:, col : col + P],
-                    rhs=x_codes[:].bitcast(FP8X4),
-                    rhs_scale=x_plane[:],
+                    rhs=x_codes.bitcast(FP8X4),
+                    rhs_scale=x_plane,
                     start=True,
                     stop=True,
                 )
-            relu = keep.tile([P, NC, C], F32, name=f"relu{e}")
-            for c in range(NC):
-                nc.scalar.activation(relu[:, c, :], y_sums[:, c, :], ACT.Relu, bias=bias[:, c, e : e + 1])
-            if e == 0:
-                for c in range(NC):
-                    nc.scalar.activation(y[:, c, slots], relu[:, c, :], ACT.Square)
-            else:
-                nc.scalar.activation(y[:, :, slots], relu[:], ACT.Square)
 
-        for e0, e1 in gather_groups:
-            if e0 > 0:
-                gather(e0, e1)
-            for e in range(e0, e1):
-                expert(e)
-
-        outs = [keep.tile([P, T], F32, name=f"out{c}") for c in range(NC)]
-        for e0, e1 in scatter_groups:
-            slots = slice(e0 * C, e1 * C)
+        def back(e0, e1):
             for c in range(NC):
-                nc.vector.tensor_tensor(outs[c][:].indirect(slot_offsets(e0, e1)), y[:, c, slots], gates[c][:, slots], ALU.mult)
+                relu = keep.tile([P, (e1 - e0) * C], F32, name=f"relu{e0}{c}", tag=f"r{c}", align_bytes=64)
+                for e in range(e0, e1):
+                    nc.scalar.activation(
+                        relu[:, (e - e0) * C : (e - e0 + 1) * C], y_sums[e][c], ACT.Relu, bias=bias[:, c, e : e + 1]
+                    )
+                y[e0, c] = keep.tile([P, (e1 - e0) * C], F32, name=f"y{e0}{c}", tag=f"y{e0}{c}", align_bytes=64)
+                nc.scalar.activation(y[e0, c][:], relu[:], ACT.Square)
+
+        def scatter(e0, e1):
+            for c in range(NC):
+                nc.vector.tensor_tensor(
+                    outs[c][:].indirect(slot_offsets(e0, e1)), y[e0, c][:], gates[:, c, e0 * C : e1 * C], ALU.mult
+                )
+
+        front(0, 1)
+        middle(0)
+        gather(1)
+        front(1, 2)
+        back(0, 1)
+        gather_late()
+        scatter(0, 1)
+        front(2, E)
+        middle(1)
+        back(1, 2)
+        middle(2)
+        middle(3)
+        back(2, E)
+        scatter(1, 2)
+        scatter(2, E)
         for c in range(NC):
             nc.sync.dma_start(out[c * P : (c + 1) * P, :], outs[c][:])

@@ -38,6 +38,9 @@ def tile_moe_prv_lin_relu2_kernel(tc, uT, wu, w_words, w_scales, b, gate, offs, 
             nc.sync.dma_start(wu_raw[h][:], wu_rows[:, :, h * (K // 2) : (h + 1) * (K // 2)])
         bias = keep.tile([P, NC, E], F32, name="bias")
         nc.sync.dma_start(bias[:], b.rearrange("(c p) e -> p c e", p=P))
+        gate_rows = gate.rearrange("(c p) s -> p c s", p=P)
+        gate_first = keep.tile([P, NC, C], F32, name="gate_first")
+        nc.sync.dma_start(gate_first[:], gate_rows[:, :, :C])
         w_codes = keep.tile([P, E * 2 * N], U8, name="w_codes", align_bytes=64)
         nc.sync.dma_start(
             w_codes[:].bitcast(I32).rearrange("p (e n) -> p e n", e=E),
@@ -50,8 +53,11 @@ def tile_moe_prv_lin_relu2_kernel(tc, uT, wu, w_words, w_scales, b, gate, offs, 
                 w_plane[32 * q : 32 * q + 4, :].bitcast(I32).rearrange("r (e n) -> r e n", e=E),
                 w_scales[:, 0, 4 * q : 4 * q + 4, :].bitcast(I32).rearrange("e r n -> r e n"),
             )
-        gates = keep.tile([P, NC, E * C], F32, name="gates")
-        nc.sync.dma_start(gates[:], gate.rearrange("(c p) s -> p c s", p=P))
+        gate_rest = keep.tile([P, NC, (E - 1) * C], F32, name="gate_rest")
+        nc.sync.dma_start(gate_rest[:], gate_rows[:, :, C:])
+
+        def gates(c, e0, e1):
+            return gate_first[:, c, :] if e0 == 0 else gate_rest[:, c, (e0 - 1) * C : (e1 - 1) * C]
 
         u_pairs = [keep.tile([P, T * 2], BF16, name=f"u_pairs{h}", align_bytes=64) for h in range(2)]
         pairs_dst = [u_pairs[h][:].rearrange("p (t j) -> p t j", j=2) for h in range(2)]
@@ -107,18 +113,18 @@ def tile_moe_prv_lin_relu2_kernel(tc, uT, wu, w_words, w_scales, b, gate, offs, 
             u_slots = keep.tile([P, 2 * C * PACK], BF16, name="u_slots2", align_bytes=64)
             rows = stage[:].bitcast(I32).rearrange("p (r s) -> p s r", r=PACK + 1)
             nc.vector.tensor_copy(u_slots[:].bitcast(I32).rearrange("p (s h) -> p s h", h=2), rows[:, :, ::PACK])
-            quantise_u(2, E, u_slots, "xp0")
+            quantise_u(2, E, u_slots, "up2")
 
         x_quantised = {}
         y_sums = {}
-        y = {}
+        factors = {}
         outs = [keep.tile([P, T], F32, name=f"out{c}") for c in range(NC)]
 
         def front(e0, e1):
             x_grouped = keep.tile([P, (e1 - e0) * C * PACK], BF16, name=f"x_grouped{e0}", align_bytes=64)
             for e in range(e0, e1):
                 u_codes, u_plane = u_quantised[e]
-                x_sums = psum.tile([P, PACK, C], F32, name=f"x_sums{e}", tag=f"xs{e}")
+                x_sums = psum.tile([P, PACK, C], F32, name=f"x_sums{e}", tag=("xs0", "xs1", "twin", "first")[e])
                 for t in range(PACK):
                     nc.tensor.matmul_mx(
                         out=x_sums[:, t, :],
@@ -138,24 +144,32 @@ def tile_moe_prv_lin_relu2_kernel(tc, uT, wu, w_words, w_scales, b, gate, offs, 
                 cols = slice((e - e0) * C, (e - e0 + 1) * C)
                 x_quantised[e] = (x_codes[:, cols], x_plane[:, cols])
 
-        def middle(e):
+        def expert_matmul(sums, e, c):
             x_codes, x_plane = x_quantised[e]
-            bank = psum.tile([P, NC, C], F32, name=f"y_sums{e}", tag=("ys0", "ys1", "ys2", "xs0")[e])
+            col = e * N + c * P
+            nc.tensor.matmul_mx(
+                out=sums,
+                lhsT=w_codes[:, 2 * col : 2 * (col + P)].bitcast(FP4X4),
+                lhsT_scale=w_plane[:, col : col + P],
+                rhs=x_codes.bitcast(FP8X4),
+                rhs_scale=x_plane,
+                start=True,
+                stop=True,
+            )
+
+        def middle(e):
+            bank = psum.tile([P, NC, C], F32, name=f"y_sums{e}", tag=f"ys{e}")
             y_sums[e] = [bank[:, c, :] for c in range(NC)]
             if e == 0:
-                first_bank = psum.tile([P, C], F32, name="y_first")
+                twin = psum.tile([P, C], F32, name="y_twin", tag="twin")
+                expert_matmul(twin[:], 0, 0)
+                gated = keep.tile([P, C], F32, name="gated")
+                nc.vector.scalar_tensor_tensor(gated[:], twin[:], bias[:, 0, 0:1], gates(0, 0, 1), ALU.add, ALU.mult)
+                factors[0, 0] = [gated[:]]
+                first_bank = psum.tile([P, C], F32, name="y_first", tag="first")
                 y_sums[e][0] = first_bank[:]
             for c in range(NC):
-                col = e * N + c * P
-                nc.tensor.matmul_mx(
-                    out=y_sums[e][c],
-                    lhsT=w_codes[:, 2 * col : 2 * (col + P)].bitcast(FP4X4),
-                    lhsT_scale=w_plane[:, col : col + P],
-                    rhs=x_codes.bitcast(FP8X4),
-                    rhs_scale=x_plane,
-                    start=True,
-                    stop=True,
-                )
+                expert_matmul(y_sums[e][c], e, c)
 
         def back(e0, e1):
             for c in range(NC):
@@ -164,14 +178,16 @@ def tile_moe_prv_lin_relu2_kernel(tc, uT, wu, w_words, w_scales, b, gate, offs, 
                     nc.scalar.activation(
                         relu[:, (e - e0) * C : (e - e0 + 1) * C], y_sums[e][c], ACT.Relu, bias=bias[:, c, e : e + 1]
                     )
-                y[e0, c] = keep.tile([P, (e1 - e0) * C], F32, name=f"y{e0}{c}", tag=f"y{e0}{c}", align_bytes=64)
-                nc.scalar.activation(y[e0, c][:], relu[:], ACT.Square)
+                if (e0, c) in factors:
+                    factors[e0, c].append(relu[:])
+                else:
+                    squared = keep.tile([P, (e1 - e0) * C], F32, name=f"y{e0}{c}", tag=f"y{e0}{c}", align_bytes=64)
+                    nc.scalar.activation(squared[:], relu[:], ACT.Square)
+                    factors[e0, c] = [squared[:], gates(c, e0, e1)]
 
         def scatter(e0, e1):
             for c in range(NC):
-                nc.vector.tensor_tensor(
-                    outs[c][:].indirect(slot_offsets(e0, e1)), y[e0, c][:], gates[:, c, e0 * C : e1 * C], ALU.mult
-                )
+                nc.vector.tensor_tensor(outs[c][:].indirect(slot_offsets(e0, e1)), *factors[e0, c], ALU.mult)
 
         front(0, 1)
         middle(0)

@@ -31,21 +31,15 @@ def tile_moe_prv_lin_relu2_kernel(tc, uT, wu, w_words, w_scales, b, gate, offs, 
         u_raw = [keep.tile([P, 2, T], F32, name=f"u_raw{h}") for h in range(2)]
         wu_rows = wu.rearrange("(p j) k -> p j k", j=PACK)
         wu_raw = [keep.tile([P, PACK, K // 2], F32, name=f"wu_raw{h}", tag=f"wu_raw{h}", align_bytes=64) for h in range(2)]
-        nc.sync.dma_start(u_raw[0][:], u_rows[:, 0:2, :])
         nc.sync.dma_start(offsets[:], offs)
+        nc.sync.dma_start(u_raw[0][:], u_rows[:, 0:2, :])
         nc.sync.dma_start(u_raw[1][:], u_rows[:, 2:4, :])
         for h in range(2):
             nc.sync.dma_start(wu_raw[h][:], wu_rows[:, :, h * (K // 2) : (h + 1) * (K // 2)])
         bias = keep.tile([P, NC, E], F32, name="bias")
         nc.sync.dma_start(bias[:], b.rearrange("(c p) e -> p c e", p=P))
-        gate_rows = gate.rearrange("(c p) s -> p c s", p=P)
-        gate_first = keep.tile([P, NC, C], F32, name="gate_first")
-        nc.sync.dma_start(gate_first[:], gate_rows[:, :, :C])
-        w_codes = keep.tile([P, E * 2 * N], U8, name="w_codes", align_bytes=64)
-        nc.sync.dma_start(
-            w_codes[:].bitcast(I32).rearrange("p (e n) -> p e n", e=E),
-            w_words[:, 0, :, :].bitcast(I32).rearrange("e p n -> p e n"),
-        )
+        gate_first = keep.tile([P, C], F32, name="gate_first")
+        nc.sync.dma_start(gate_first[:], gate[:P, :C])
         w_plane = keep.tile([P, E * N], U8, name="w_plane", align_bytes=64)
         nc.gpsimd.memset(w_plane[:].bitcast(I32), 0)
         for q in range(4):
@@ -53,50 +47,73 @@ def tile_moe_prv_lin_relu2_kernel(tc, uT, wu, w_words, w_scales, b, gate, offs, 
                 w_plane[32 * q : 32 * q + 4, :].bitcast(I32).rearrange("r (e n) -> r e n", e=E),
                 w_scales[:, 0, 4 * q : 4 * q + 4, :].bitcast(I32).rearrange("e r n -> r e n"),
             )
-        gate_rest = keep.tile([P, NC, (E - 1) * C], F32, name="gate_rest")
-        nc.sync.dma_start(gate_rest[:], gate_rows[:, :, C:])
+        w_codes = keep.tile([P, E * 2 * N], U8, name="w_codes", align_bytes=64)
+        nc.sync.dma_start(
+            w_codes[:].bitcast(I32).rearrange("p (e n) -> p e n", e=E),
+            w_words[:, 0, :, :].bitcast(I32).rearrange("e p n -> p e n"),
+        )
+        gate_rest = keep.tile([P, E * C], F32, name="gate_rest")
+        nc.sync.dma_start(gate_rest[:], gate[P : 2 * P, :])
 
         def gates(c, e0, e1):
-            return gate_first[:, c, :] if e0 == 0 else gate_rest[:, c, (e0 - 1) * C : (e1 - 1) * C]
+            return gate_first[:] if e1 == 1 else gate_rest[:, e0 * C : e1 * C]
 
         u_pairs = [keep.tile([P, T * 2], BF16, name=f"u_pairs{h}", align_bytes=64) for h in range(2)]
-        pairs_dst = [u_pairs[h][:].rearrange("p (t j) -> p t j", j=2) for h in range(2)]
-        pairs_src = [u_raw[h][:].rearrange("p j t -> p t j") for h in range(2)]
-        nc.vector.tensor_copy(pairs_dst[0][:, :336], pairs_src[0][:, :336])
-        nc.scalar.copy(pairs_dst[0][:, 336:], pairs_src[0][:, 336:])
-        nc.scalar.copy(pairs_dst[1], pairs_src[1])
+
+        def cast_u(h, share):
+            dst = u_pairs[h][:].rearrange("p (t j) -> p t j", j=2)
+            src = u_raw[h][:].rearrange("p j t -> p t j")
+            nc.vector.tensor_copy(dst[:, :share], src[:, :share])
+            nc.scalar.copy(dst[:, share:], src[:, share:])
 
         def slot_offsets(e0, e1):
             return offsets[:, e0 * (C // 16) : e1 * (C // 16)]
 
+        block = P * PACK
+        later = T - C
+        early = 2 * (later + C)
+        stage = keep.tile([P, early + PACK * block], BF16, name="stage", align_bytes=64)
+        wu_grouped = stage[:, early:]
+
+        def gather(h, e0, e1):
+            row = stage[:, 2 * (h * later + (e0 - 1) * C) : 2 * (h * later + (e1 - 1) * C)]
+            nc.vector.tensor_copy(row.bitcast(U32), u_pairs[h][:].bitcast(U32).indirect(slot_offsets(e0, e1)))
+
+        u_slots = {0: keep.tile([P, C * PACK], BF16, name="u_slots0", align_bytes=64)}
+
+        def gather_first(h):
+            words = u_slots[0][:].bitcast(U32).rearrange("p (s h) -> p s h", h=2)
+            nc.vector.tensor_copy(words[:, :, h], u_pairs[h][:].bitcast(U32).indirect(slot_offsets(0, 1)))
+
+        def weave(copy, dtype, e0, e1, tag):
+            u_slots[e0] = keep.tile([P, (e1 - e0) * C * PACK], BF16, name=f"u_slots{e0}", tag=tag, align_bytes=64)
+            rows = stage[:, : 4 * later].bitcast(dtype).rearrange("p (h s) -> p s h", h=2)
+            copy(u_slots[e0][:].bitcast(dtype).rearrange("p (s h) -> p s h", h=2), rows[:, (e0 - 1) * C : (e1 - 1) * C, :])
+
         u_quantised = {}
 
-        def quantise_u(e0, e1, u_slots, plane_tag):
+        def quantise_u(e0, e1):
             u_codes = keep.tile([P, (e1 - e0) * C], U32, name=f"u_codes{e0}", align_bytes=64)
-            u_plane = keep.tile([P, (e1 - e0) * C], U8, name=f"u_plane{e0}", tag=plane_tag, align_bytes=64)
-            nc.vector.quantize_mx(out=u_codes[:].bitcast(FP8X4), scales=u_plane[:], in_=u_slots[:])
+            u_plane = keep.tile([P, (e1 - e0) * C], U8, name=f"u_plane{e0}", align_bytes=64)
+            nc.vector.quantize_mx(out=u_codes[:].bitcast(FP8X4), scales=u_plane[:], in_=u_slots[e0][:])
             for e in range(e0, e1):
                 cols = slice((e - e0) * C, (e - e0 + 1) * C)
                 u_quantised[e] = (u_codes[:, cols], u_plane[:, cols])
 
-        def gather(e):
-            u_slots = keep.tile([P, C * PACK], BF16, name=f"u_slots{e}", align_bytes=64)
-            words = u_slots[:].bitcast(U32).rearrange("p (s h) -> p s h", h=2)
-            for h in range(2):
-                nc.vector.tensor_copy(words[:, :, h], u_pairs[h][:].bitcast(U32).indirect(slot_offsets(e, e + 1)))
-            quantise_u(e, e + 1, u_slots, ("up0", "wu_raw1")[e])
+        cast_u(0, 336)
+        gather_first(0)
+        gather(0, 1, E)
+        cast_u(1, 192)
+        gather_first(1)
+        gather(1, 1, 2)
+        quantise_u(0, 1)
 
-        gather(0)
-
-        block = P * PACK
-        stage = keep.tile([P, (PACK + 1) * block], BF16, name="stage", align_bytes=64)
-        wu_grouped = stage[:, block:]
         wu_dst = wu_grouped.rearrange("p (t m j) -> p m t j", t=PACK, j=PACK)
         half = P // 2
         wu_src = [wu_raw[h][:].rearrange("p j (m t) -> p m t j", t=PACK) for h in range(2)]
         nc.scalar.copy(wu_dst[:, :half], wu_src[0])
-        nc.vector.tensor_copy(wu_dst[:, half : half + 56], wu_src[1][:, :56])
-        nc.scalar.copy(wu_dst[:, half + 56 :], wu_src[1][:, 56:])
+        nc.vector.tensor_copy(wu_dst[:, half : half + 48], wu_src[1][:, :48])
+        nc.scalar.copy(wu_dst[:, half + 48 :], wu_src[1][:, 48:])
         wu_codes = keep.tile([P, K], U32, name="wu_codes", align_bytes=64)
         wu_plane = keep.tile([P, K], U8, name="wu_plane", align_bytes=64)
         for t in range(PACK):
@@ -105,26 +122,20 @@ def tile_moe_prv_lin_relu2_kernel(tc, uT, wu, w_words, w_scales, b, gate, offs, 
                 scales=wu_plane[:, t * P : (t + 1) * P],
                 in_=wu_grouped[:, t * block : (t + 1) * block],
             )
-
-        def gather_late():
-            for h in range(2):
-                row = stage[:, h * PACK * block : (h * PACK + 1) * block]
-                nc.vector.tensor_copy(row.bitcast(U32), u_pairs[h][:].bitcast(U32).indirect(slot_offsets(2, E)))
-            u_slots = keep.tile([P, 2 * C * PACK], BF16, name="u_slots2", align_bytes=64)
-            rows = stage[:].bitcast(I32).rearrange("p (r s) -> p s r", r=PACK + 1)
-            nc.vector.tensor_copy(u_slots[:].bitcast(I32).rearrange("p (s h) -> p s h", h=2), rows[:, :, ::PACK])
-            quantise_u(2, E, u_slots, "up2")
+        weave(nc.scalar.copy, U32, 1, 2, "wu_raw1")
+        quantise_u(1, 2)
+        gather(1, 2, E)
 
         x_quantised = {}
         y_sums = {}
         factors = {}
-        outs = [keep.tile([P, T], F32, name=f"out{c}") for c in range(NC)]
+        outs = {}
 
         def front(e0, e1):
-            x_grouped = keep.tile([P, (e1 - e0) * C * PACK], BF16, name=f"x_grouped{e0}", align_bytes=64)
+            x_grouped = keep.tile([P, (e1 - e0) * C * PACK], BF16, name=f"x_grouped{e0}", tag=f"xg{e0}", align_bytes=64)
             for e in range(e0, e1):
                 u_codes, u_plane = u_quantised[e]
-                x_sums = psum.tile([P, PACK, C], F32, name=f"x_sums{e}", tag=("xs0", "xs1", "twin", "first")[e])
+                x_sums = psum.tile([P, PACK, C], F32, name=f"x_sums{e}", tag=("xs0", "xs1", "first", "twin")[e])
                 for t in range(PACK):
                     nc.tensor.matmul_mx(
                         out=x_sums[:, t, :],
@@ -137,7 +148,7 @@ def tile_moe_prv_lin_relu2_kernel(tc, uT, wu, w_words, w_scales, b, gate, offs, 
                     )
                 part = x_grouped[:, (e - e0) * C * PACK : (e - e0 + 1) * C * PACK]
                 nc.scalar.copy(part.rearrange("p (s t) -> p s t", t=PACK), x_sums[:].rearrange("p t s -> p s t"))
-            x_codes = keep.tile([P, (e1 - e0) * C], U32, name=f"x_codes{e0}", tag=("xc0", "xc1", "y01")[e0], align_bytes=64)
+            x_codes = keep.tile([P, (e1 - e0) * C], U32, name=f"x_codes{e0}", align_bytes=64)
             x_plane = keep.tile([P, (e1 - e0) * C], U8, name=f"x_plane{e0}", tag=f"xp{e0}", align_bytes=64)
             nc.vector.quantize_mx(out=x_codes[:].bitcast(FP8X4), scales=x_plane[:], in_=x_grouped[:])
             for e in range(e0, e1):
@@ -157,52 +168,61 @@ def tile_moe_prv_lin_relu2_kernel(tc, uT, wu, w_words, w_scales, b, gate, offs, 
                 stop=True,
             )
 
-        def middle(e):
-            bank = psum.tile([P, NC, C], F32, name=f"y_sums{e}", tag=f"ys{e}")
-            y_sums[e] = [bank[:, c, :] for c in range(NC)]
-            if e == 0:
-                twin = psum.tile([P, C], F32, name="y_twin", tag="twin")
-                expert_matmul(twin[:], 0, 0)
-                gated = keep.tile([P, C], F32, name="gated")
-                nc.vector.scalar_tensor_tensor(gated[:], twin[:], bias[:, 0, 0:1], gates(0, 0, 1), ALU.add, ALU.mult)
-                factors[0, 0] = [gated[:]]
-                first_bank = psum.tile([P, C], F32, name="y_first", tag="first")
-                y_sums[e][0] = first_bank[:]
-            for c in range(NC):
-                expert_matmul(y_sums[e][c], e, c)
+        def middle(e0, e1, c, tag):
+            bank = psum.tile([P, (e1 - e0) * C], F32, name=f"y_sums{e0}{c}", tag=tag)
+            for e in range(e0, e1):
+                y_sums[e, c] = bank[:, (e - e0) * C : (e - e0 + 1) * C]
+                expert_matmul(y_sums[e, c], e, c)
 
-        def back(e0, e1):
-            for c in range(NC):
-                relu = keep.tile([P, (e1 - e0) * C], F32, name=f"relu{e0}{c}", tag=f"r{c}", align_bytes=64)
-                for e in range(e0, e1):
-                    nc.scalar.activation(
-                        relu[:, (e - e0) * C : (e - e0 + 1) * C], y_sums[e][c], ACT.Relu, bias=bias[:, c, e : e + 1]
-                    )
-                if (e0, c) in factors:
-                    factors[e0, c].append(relu[:])
-                else:
-                    squared = keep.tile([P, (e1 - e0) * C], F32, name=f"y{e0}{c}", tag=f"y{e0}{c}", align_bytes=64)
-                    nc.scalar.activation(squared[:], relu[:], ACT.Square)
-                    factors[e0, c] = [squared[:], gates(c, e0, e1)]
+        def twin_chunk():
+            twin = psum.tile([P, C], F32, name="y_twin", tag="twin")
+            expert_matmul(twin[:], 0, 0)
+            gated = keep.tile([P, C], F32, name="gated")
+            nc.vector.scalar_tensor_tensor(gated[:], twin[:], bias[:, 0, 0:1], gates(0, 0, 1), ALU.add, ALU.mult)
+            factors[0, 0] = [gated[:]]
 
-        def scatter(e0, e1):
-            for c in range(NC):
-                nc.vector.tensor_tensor(outs[c][:].indirect(slot_offsets(e0, e1)), *factors[e0, c], ALU.mult)
+        def back(e0, e1, c):
+            relu = keep.tile([P, (e1 - e0) * C], F32, name=f"relu{e0}{c}", align_bytes=64)
+            for e in range(e0, e1):
+                nc.scalar.activation(
+                    relu[:, (e - e0) * C : (e - e0 + 1) * C], y_sums[e, c], ACT.Relu, bias=bias[:, c, e : e + 1]
+                )
+            if (e0, c) in factors:
+                factors[e0, c].append(relu[:])
+            else:
+                squared = keep.tile([P, (e1 - e0) * C], F32, name=f"y{e0}{c}", align_bytes=64)
+                nc.scalar.activation(squared[:], relu[:], ACT.Square)
+                factors[e0, c] = [squared[:], gates(c, e0, e1)]
+
+        def scatter(e0, e1, c):
+            if c not in outs:
+                outs[c] = keep.tile([P, T], F32, name=f"out{c}", tag=("out0", "out1", "xg2")[c], align_bytes=64)
+            nc.vector.tensor_tensor(outs[c][:].indirect(slot_offsets(e0, e1)), *factors[e0, c], ALU.mult)
 
         front(0, 1)
-        middle(0)
-        gather(1)
+        weave(nc.vector.tensor_copy, I32, 2, E, "xg0")
+        twin_chunk()
+        middle(0, 1, 0, "first")
+        middle(0, 1, 1, "y01")
         front(1, 2)
-        back(0, 1)
-        gather_late()
-        scatter(0, 1)
+        quantise_u(2, E)
+        back(0, 1, 0)
+        scatter(0, 1, 0)
+        middle(1, 2, 0, "y10")
+        middle(0, 2, 2, "y02")
+        back(0, 1, 1)
+        scatter(0, 1, 1)
+        back(1, 2, 0)
+        scatter(1, 2, 0)
         front(2, E)
-        middle(1)
-        back(1, 2)
-        middle(2)
-        middle(3)
-        back(2, E)
-        scatter(1, 2)
-        scatter(2, E)
+        middle(1, 2, 1, "twin")
+        back(0, 2, 2)
+        scatter(0, 2, 2)
+        back(1, 2, 1)
+        scatter(1, 2, 1)
+        for c in range(NC):
+            middle(2, E, c, ("xs0", "xs1", "first")[c])
+            back(2, E, c)
+            scatter(2, E, c)
         for c in range(NC):
             nc.sync.dma_start(out[c * P : (c + 1) * P, :], outs[c][:])

@@ -28,14 +28,24 @@ def tile_moe_prv_lin_relu2_kernel(tc, uT, wu, w_words, w_scales, b, gate, offs, 
 
         offsets = keep.tile([P, E * C // 16], U16, name="offsets")
         u_rows = uT.rearrange("(p j) t -> p j t", j=PACK)
-        u_raw = [keep.tile([P, 2, T], F32, name=f"u_raw{h}") for h in range(2)]
+        block = P * PACK
+        later = T - 2 * C
+        early = 2 * later
+        stage = keep.tile([P, early + PACK * block], BF16, name="stage", align_bytes=64)
+        wu_grouped = stage[:, early:]
+        u_first = keep.tile([P, 2, T], F32, name="u_first", tag="u_raw0", align_bytes=64)
+        u_raw = [u_first[:], wu_grouped.bitcast(F32).rearrange("p (j t) -> p j t", j=2)]
         wu_rows = wu.rearrange("(p j) k -> p j k", j=PACK)
-        wu_raw = [keep.tile([P, PACK, K // 2], F32, name=f"wu_raw{h}", tag=f"wu_raw{h}", align_bytes=64) for h in range(2)]
+        reuse = ctx.enter_context(tc.tile_pool(name="reuse", bufs=1))
+        wu_raw = [
+            keep.tile([P, PACK, K // 2], F32, name="wu_raw0", align_bytes=64),
+            reuse.tile([P, PACK, K // 2], F32, name="wu_raw1", align_bytes=64, offset=0),
+        ]
         nc.sync.dma_start(offsets[:], offs)
-        nc.sync.dma_start(u_raw[0][:], u_rows[:, 0:2, :])
-        nc.sync.dma_start(u_raw[1][:], u_rows[:, 2:4, :])
+        nc.sync.dma_start(u_raw[0], u_rows[:, 0:2, :])
+        nc.sync.dma_start(u_raw[1], u_rows[:, 2:4, :])
         for h in range(2):
-            nc.sync.dma_start(wu_raw[h][:], wu_rows[:, :, h * (K // 2) : (h + 1) * (K // 2)])
+            nc.sync.dma_start(wu_raw[h], wu_rows[:, :, h * (K // 2) : (h + 1) * (K // 2)])
         bias = keep.tile([P, NC, E], F32, name="bias")
         nc.sync.dma_start(bias[:], b.rearrange("(c p) e -> p c e", p=P))
         gate_first = keep.tile([P, C], F32, name="gate_first")
@@ -58,62 +68,62 @@ def tile_moe_prv_lin_relu2_kernel(tc, uT, wu, w_words, w_scales, b, gate, offs, 
         def gates(c, e0, e1):
             return gate_first[:] if e1 == 1 else gate_rest[:, e0 * C : e1 * C]
 
-        u_pairs = [keep.tile([P, T * 2], BF16, name=f"u_pairs{h}", align_bytes=64) for h in range(2)]
+        u_pairs = [keep.tile([P, T * 2], BF16, name=f"u_pairs{h}", tag=("pairs0", "u_raw0")[h], align_bytes=64) for h in range(2)]
 
         def cast_u(h, share):
             dst = u_pairs[h][:].rearrange("p (t j) -> p t j", j=2)
-            src = u_raw[h][:].rearrange("p j t -> p t j")
+            src = u_raw[h].rearrange("p j t -> p t j")
             nc.vector.tensor_copy(dst[:, :share], src[:, :share])
             nc.scalar.copy(dst[:, share:], src[:, share:])
 
         def slot_offsets(e0, e1):
             return offsets[:, e0 * (C // 16) : e1 * (C // 16)]
 
-        block = P * PACK
-        later = T - C
-        early = 2 * (later + C)
-        stage = keep.tile([P, early + PACK * block], BF16, name="stage", align_bytes=64)
-        wu_grouped = stage[:, early:]
 
         def gather(h, e0, e1):
-            row = stage[:, 2 * (h * later + (e0 - 1) * C) : 2 * (h * later + (e1 - 1) * C)]
+            row = stage[:, 2 * (h * later + (e0 - 2) * C) : 2 * (h * later + (e1 - 2) * C)]
             nc.vector.tensor_copy(row.bitcast(U32), u_pairs[h][:].bitcast(U32).indirect(slot_offsets(e0, e1)))
 
-        u_slots = {0: keep.tile([P, C * PACK], BF16, name="u_slots0", align_bytes=64)}
+        first_slots = keep.tile([P, 2 * C * PACK], BF16, name="first_slots", align_bytes=64)
+        u_slots = {e: first_slots[:, e * C * PACK : (e + 1) * C * PACK] for e in range(2)}
 
         def gather_first(h):
-            words = u_slots[0][:].bitcast(U32).rearrange("p (s h) -> p s h", h=2)
-            nc.vector.tensor_copy(words[:, :, h], u_pairs[h][:].bitcast(U32).indirect(slot_offsets(0, 1)))
+            words = first_slots[:].bitcast(U32).rearrange("p (s h) -> p s h", h=2)
+            nc.vector.tensor_copy(words[:, :, h], u_pairs[h][:].bitcast(U32).indirect(slot_offsets(0, 2)))
 
-        def weave(copy, dtype, e0, e1, tag):
-            u_slots[e0] = keep.tile([P, (e1 - e0) * C * PACK], BF16, name=f"u_slots{e0}", tag=tag, align_bytes=64)
+        def weave(copy, dtype, e0, e1, woven):
+            u_slots[e0] = woven[:]
             rows = stage[:, : 4 * later].bitcast(dtype).rearrange("p (h s) -> p s h", h=2)
-            copy(u_slots[e0][:].bitcast(dtype).rearrange("p (s h) -> p s h", h=2), rows[:, (e0 - 1) * C : (e1 - 1) * C, :])
+            copy(u_slots[e0].bitcast(dtype).rearrange("p (s h) -> p s h", h=2), rows[:, (e0 - 2) * C : (e1 - 2) * C, :])
 
         u_quantised = {}
 
-        def quantise_u(e0, e1):
-            u_codes = keep.tile([P, (e1 - e0) * C], U32, name=f"u_codes{e0}", align_bytes=64)
-            u_plane = keep.tile([P, (e1 - e0) * C], U8, name=f"u_plane{e0}", align_bytes=64)
-            nc.vector.quantize_mx(out=u_codes[:].bitcast(FP8X4), scales=u_plane[:], in_=u_slots[e0][:])
+        def quantise_u(e0, e1, u_codes):
+            if e0 == 0:
+                u_plane = keep.tile([P, C], U8, name="u_plane0", align_bytes=64)[:]
+            elif e0 == 1:
+                u_plane = reuse.tile([P, C], U8, name="u_plane1", align_bytes=64, offset=0)[:]
+            else:
+                u_plane = w_codes[:, : 2 * P]
+            nc.vector.quantize_mx(out=u_codes[:].bitcast(FP8X4), scales=u_plane, in_=u_slots[e0])
             for e in range(e0, e1):
                 cols = slice((e - e0) * C, (e - e0 + 1) * C)
                 u_quantised[e] = (u_codes[:, cols], u_plane[:, cols])
 
         cast_u(0, 336)
         gather_first(0)
-        gather(0, 1, E)
-        cast_u(1, 192)
+        cast_u(1, 224)
+        gather(0, 2, E)
         gather_first(1)
-        gather(1, 1, 2)
-        quantise_u(0, 1)
+        quantise_u(0, 1, keep.tile([P, C], U32, name="u_codes0", align_bytes=64))
 
-        wu_dst = wu_grouped.rearrange("p (t m j) -> p m t j", t=PACK, j=PACK)
+        wu_dst = wu_grouped.rearrange("p (t m j) -> p m j t", t=PACK, j=PACK)
         half = P // 2
-        wu_src = [wu_raw[h][:].rearrange("p j (m t) -> p m t j", t=PACK) for h in range(2)]
+        wu_src = [wu_raw[h][:].rearrange("p j (m t) -> p m j t", t=PACK) for h in range(2)]
         nc.scalar.copy(wu_dst[:, :half], wu_src[0])
-        nc.vector.tensor_copy(wu_dst[:, half : half + 48], wu_src[1][:, :48])
-        nc.scalar.copy(wu_dst[:, half + 48 :], wu_src[1][:, 48:])
+        for t in range(0, PACK, 2):
+            nc.vector.tensor_copy(wu_dst[:, half : half + 48, :, t : t + 2], wu_src[1][:, :48, :, t : t + 2])
+            nc.scalar.copy(wu_dst[:, half + 48 :, :, t : t + 2], wu_src[1][:, 48:, :, t : t + 2])
         wu_codes = keep.tile([P, K], U32, name="wu_codes", align_bytes=64)
         wu_plane = keep.tile([P, K], U8, name="wu_plane", align_bytes=64)
         for t in range(PACK):
@@ -122,8 +132,7 @@ def tile_moe_prv_lin_relu2_kernel(tc, uT, wu, w_words, w_scales, b, gate, offs, 
                 scales=wu_plane[:, t * P : (t + 1) * P],
                 in_=wu_grouped[:, t * block : (t + 1) * block],
             )
-        weave(nc.scalar.copy, U32, 1, 2, "wu_raw1")
-        quantise_u(1, 2)
+        quantise_u(1, 2, keep.tile([P, C], U32, name="u_codes1", align_bytes=64))
         gather(1, 2, E)
 
         x_quantised = {}
@@ -135,19 +144,22 @@ def tile_moe_prv_lin_relu2_kernel(tc, uT, wu, w_words, w_scales, b, gate, offs, 
             x_grouped = keep.tile([P, (e1 - e0) * C * PACK], BF16, name=f"x_grouped{e0}", tag=f"xg{e0}", align_bytes=64)
             for e in range(e0, e1):
                 u_codes, u_plane = u_quantised[e]
-                x_sums = psum.tile([P, PACK, C], F32, name=f"x_sums{e}", tag=("xs0", "xs1", "first", "twin")[e])
-                for t in range(PACK):
-                    nc.tensor.matmul_mx(
-                        out=x_sums[:, t, :],
-                        lhsT=wu_codes[:, t * P : (t + 1) * P].bitcast(FP8X4),
-                        lhsT_scale=wu_plane[:, t * P : (t + 1) * P],
-                        rhs=u_codes.bitcast(FP8X4),
-                        rhs_scale=u_plane,
-                        start=True,
-                        stop=True,
-                    )
-                part = x_grouped[:, (e - e0) * C * PACK : (e - e0 + 1) * C * PACK]
-                nc.scalar.copy(part.rearrange("p (s t) -> p s t", t=PACK), x_sums[:].rearrange("p t s -> p s t"))
+                part = x_grouped[:, (e - e0) * C * PACK : (e - e0 + 1) * C * PACK].rearrange("p (s t) -> p s t", t=PACK)
+                tags = (("xs0", "xs0b"), ("xs1",), ("first",), ("twin",))[e]
+                width = PACK // len(tags)
+                for i, tag in enumerate(tags):
+                    x_sums = psum.tile([P, width, C], F32, name=f"x_sums{e}{i}", tag=tag)
+                    for t in range(i * width, (i + 1) * width):
+                        nc.tensor.matmul_mx(
+                            out=x_sums[:, t - i * width, :],
+                            lhsT=wu_codes[:, t * P : (t + 1) * P].bitcast(FP8X4),
+                            lhsT_scale=wu_plane[:, t * P : (t + 1) * P],
+                            rhs=u_codes.bitcast(FP8X4),
+                            rhs_scale=u_plane,
+                            start=True,
+                            stop=True,
+                        )
+                    nc.scalar.copy(part[:, :, i * width : (i + 1) * width], x_sums[:].rearrange("p t s -> p s t"))
             x_codes = keep.tile([P, (e1 - e0) * C], U32, name=f"x_codes{e0}", align_bytes=64)
             x_plane = keep.tile([P, (e1 - e0) * C], U8, name=f"x_plane{e0}", tag=f"xp{e0}", align_bytes=64)
             nc.vector.quantize_mx(out=x_codes[:].bitcast(FP8X4), scales=x_plane[:], in_=x_grouped[:])
@@ -200,12 +212,12 @@ def tile_moe_prv_lin_relu2_kernel(tc, uT, wu, w_words, w_scales, b, gate, offs, 
             nc.vector.tensor_tensor(outs[c][:].indirect(slot_offsets(e0, e1)), *factors[e0, c], ALU.mult)
 
         front(0, 1)
-        weave(nc.vector.tensor_copy, I32, 2, E, "xg0")
-        twin_chunk()
+        weave(nc.vector.tensor_copy, I32, 2, E, keep.tile([P, 2 * C * PACK], BF16, name="u_slots2", tag="xg0", align_bytes=64))
         middle(0, 1, 0, "first")
+        twin_chunk()
+        quantise_u(2, E, keep.tile([P, 2 * C], U32, name="u_codes2", align_bytes=64))
         middle(0, 1, 1, "y01")
         front(1, 2)
-        quantise_u(2, E)
         back(0, 1, 0)
         scatter(0, 1, 0)
         middle(1, 2, 0, "y10")

@@ -29,8 +29,8 @@ def tile_moe_prv_lin_relu2_kernel(tc, uT, wu, w_words, w_scales, b, gate, offs, 
         offsets = keep.tile([P, E * C // 16], U16, name="offsets")
         u_rows = uT.rearrange("(p j) t -> p j t", j=PACK)
         block = P * PACK
-        later = T - 2 * C
-        early = 2 * later
+        later = T - C
+        early = 2 * (later + C)
         stage = keep.tile([P, early + PACK * block], BF16, name="stage", align_bytes=64)
         wu_grouped = stage[:, early:]
         u_first = keep.tile([P, 2, T], F32, name="u_first", tag="u_raw0", align_bytes=64)
@@ -41,8 +41,8 @@ def tile_moe_prv_lin_relu2_kernel(tc, uT, wu, w_words, w_scales, b, gate, offs, 
             keep.tile([P, PACK, K // 2], F32, name="wu_raw0", align_bytes=64),
             reuse.tile([P, PACK, K // 2], F32, name="wu_raw1", align_bytes=64, offset=0),
         ]
-        nc.sync.dma_start(offsets[:], offs)
         nc.sync.dma_start(u_raw[0], u_rows[:, 0:2, :])
+        nc.sync.dma_start(offsets[:], offs)
         nc.sync.dma_start(u_raw[1], u_rows[:, 2:4, :])
         for h in range(2):
             nc.sync.dma_start(wu_raw[h], wu_rows[:, :, h * (K // 2) : (h + 1) * (K // 2)])
@@ -62,11 +62,11 @@ def tile_moe_prv_lin_relu2_kernel(tc, uT, wu, w_words, w_scales, b, gate, offs, 
             w_codes[:].bitcast(I32).rearrange("p (e n) -> p e n", e=E),
             w_words[:, 0, :, :].bitcast(I32).rearrange("e p n -> p e n"),
         )
-        gate_rest = keep.tile([P, E * C], F32, name="gate_rest")
-        nc.sync.dma_start(gate_rest[:], gate[P : 2 * P, :])
+        gate_rest = keep.tile([P, (E - 1) * C], F32, name="gate_rest")
+        nc.sync.dma_start(gate_rest[:], gate[:P, C:])
 
         def gates(c, e0, e1):
-            return gate_first[:] if e1 == 1 else gate_rest[:, e0 * C : e1 * C]
+            return gate_first[:] if e1 == 1 else gate_rest[:, (e0 - 1) * C : (e1 - 1) * C]
 
         u_pairs = [keep.tile([P, T * 2], BF16, name=f"u_pairs{h}", tag=("pairs0", "u_raw0")[h], align_bytes=64) for h in range(2)]
 
@@ -81,20 +81,20 @@ def tile_moe_prv_lin_relu2_kernel(tc, uT, wu, w_words, w_scales, b, gate, offs, 
 
 
         def gather(h, e0, e1):
-            row = stage[:, 2 * (h * later + (e0 - 2) * C) : 2 * (h * later + (e1 - 2) * C)]
+            row = stage[:, 2 * (h * later + (e0 - 1) * C) : 2 * (h * later + (e1 - 1) * C)]
             nc.vector.tensor_copy(row.bitcast(U32), u_pairs[h][:].bitcast(U32).indirect(slot_offsets(e0, e1)))
 
-        first_slots = keep.tile([P, 2 * C * PACK], BF16, name="first_slots", align_bytes=64)
-        u_slots = {e: first_slots[:, e * C * PACK : (e + 1) * C * PACK] for e in range(2)}
+        first_slots = keep.tile([P, C * PACK], BF16, name="first_slots", align_bytes=64)
+        u_slots = {0: first_slots[:]}
 
         def gather_first(h):
             words = first_slots[:].bitcast(U32).rearrange("p (s h) -> p s h", h=2)
-            nc.vector.tensor_copy(words[:, :, h], u_pairs[h][:].bitcast(U32).indirect(slot_offsets(0, 2)))
+            nc.vector.tensor_copy(words[:, :, h], u_pairs[h][:].bitcast(U32).indirect(slot_offsets(0, 1)))
 
         def weave(copy, dtype, e0, e1, woven):
             u_slots[e0] = woven[:]
             rows = stage[:, : 4 * later].bitcast(dtype).rearrange("p (h s) -> p s h", h=2)
-            copy(u_slots[e0].bitcast(dtype).rearrange("p (s h) -> p s h", h=2), rows[:, (e0 - 2) * C : (e1 - 2) * C, :])
+            copy(u_slots[e0].bitcast(dtype).rearrange("p (s h) -> p s h", h=2), rows[:, (e0 - 1) * C : (e1 - 1) * C, :])
 
         u_quantised = {}
 
@@ -102,9 +102,9 @@ def tile_moe_prv_lin_relu2_kernel(tc, uT, wu, w_words, w_scales, b, gate, offs, 
             if e0 == 0:
                 u_plane = keep.tile([P, C], U8, name="u_plane0", align_bytes=64)[:]
             elif e0 == 1:
-                u_plane = reuse.tile([P, C], U8, name="u_plane1", align_bytes=64, offset=0)[:]
+                u_plane = keep.tile([P, C], U8, name="u_plane1", align_bytes=64)[:]
             else:
-                u_plane = w_codes[:, : 2 * P]
+                u_plane = keep.tile([P, 2 * C], U8, name="u_plane2", align_bytes=64)[:]
             nc.vector.quantize_mx(out=u_codes[:].bitcast(FP8X4), scales=u_plane, in_=u_slots[e0])
             for e in range(e0, e1):
                 cols = slice((e - e0) * C, (e - e0 + 1) * C)
@@ -112,9 +112,10 @@ def tile_moe_prv_lin_relu2_kernel(tc, uT, wu, w_words, w_scales, b, gate, offs, 
 
         cast_u(0, 336)
         gather_first(0)
-        cast_u(1, 224)
-        gather(0, 2, E)
+        cast_u(1, 96)
+        gather(0, 1, E)
         gather_first(1)
+        gather(1, 1, 2)
         quantise_u(0, 1, keep.tile([P, C], U32, name="u_codes0", align_bytes=64))
 
         wu_dst = wu_grouped.rearrange("p (t m j) -> p m j t", t=PACK, j=PACK)
@@ -132,8 +133,10 @@ def tile_moe_prv_lin_relu2_kernel(tc, uT, wu, w_words, w_scales, b, gate, offs, 
                 scales=wu_plane[:, t * P : (t + 1) * P],
                 in_=wu_grouped[:, t * block : (t + 1) * block],
             )
-        quantise_u(1, 2, keep.tile([P, C], U32, name="u_codes1", align_bytes=64))
+        weave(nc.scalar.copy, U32, 1, 2, reuse.tile([P, C * PACK], BF16, name="u_slots1", align_bytes=64, offset=0))
         gather(1, 2, E)
+        quantise_u(1, 2, keep.tile([P, C], U32, name="u_codes1", align_bytes=64))
+        weave(nc.vector.tensor_copy, I32, 2, E, keep.tile([P, 2 * C * PACK], BF16, name="u_slots2", align_bytes=64))
 
         x_quantised = {}
         y_sums = {}
@@ -161,8 +164,11 @@ def tile_moe_prv_lin_relu2_kernel(tc, uT, wu, w_words, w_scales, b, gate, offs, 
                         )
                     nc.scalar.copy(part[:, :, i * width : (i + 1) * width], x_sums[:].rearrange("p t s -> p s t"))
             x_codes = keep.tile([P, (e1 - e0) * C], U32, name=f"x_codes{e0}", align_bytes=64)
-            x_plane = keep.tile([P, (e1 - e0) * C], U8, name=f"x_plane{e0}", tag=f"xp{e0}", align_bytes=64)
-            nc.vector.quantize_mx(out=x_codes[:].bitcast(FP8X4), scales=x_plane[:], in_=x_grouped[:])
+            if e0 == 1:
+                x_plane = w_codes[:, :C]
+            else:
+                x_plane = keep.tile([P, (e1 - e0) * C], U8, name=f"x_plane{e0}", align_bytes=64)[:]
+            nc.vector.quantize_mx(out=x_codes[:].bitcast(FP8X4), scales=x_plane, in_=x_grouped[:])
             for e in range(e0, e1):
                 cols = slice((e - e0) * C, (e - e0 + 1) * C)
                 x_quantised[e] = (x_codes[:, cols], x_plane[:, cols])
@@ -208,32 +214,28 @@ def tile_moe_prv_lin_relu2_kernel(tc, uT, wu, w_words, w_scales, b, gate, offs, 
 
         def scatter(e0, e1, c):
             if c not in outs:
-                outs[c] = keep.tile([P, T], F32, name=f"out{c}", tag=("out0", "out1", "xg2")[c], align_bytes=64)
+                outs[c] = keep.tile([P, T], F32, name=f"out{c}", align_bytes=64)
             nc.vector.tensor_tensor(outs[c][:].indirect(slot_offsets(e0, e1)), *factors[e0, c], ALU.mult)
 
         front(0, 1)
-        weave(nc.vector.tensor_copy, I32, 2, E, keep.tile([P, 2 * C * PACK], BF16, name="u_slots2", tag="xg0", align_bytes=64))
+        quantise_u(2, E, keep.tile([P, 2 * C], U32, name="u_codes2", tag="xg0", align_bytes=64))
         middle(0, 1, 0, "first")
         twin_chunk()
-        quantise_u(2, E, keep.tile([P, 2 * C], U32, name="u_codes2", align_bytes=64))
         middle(0, 1, 1, "y01")
-        front(1, 2)
+        middle(0, 1, 2, "y02")
         back(0, 1, 0)
+        front(1, 2)
         scatter(0, 1, 0)
-        middle(1, 2, 0, "y10")
-        middle(0, 2, 2, "y02")
-        back(0, 1, 1)
-        scatter(0, 1, 1)
-        back(1, 2, 0)
-        scatter(1, 2, 0)
+        for c in range(1, NC):
+            back(0, 1, c)
+            scatter(0, 1, c)
         front(2, E)
-        middle(1, 2, 1, "twin")
-        back(0, 2, 2)
-        scatter(0, 2, 2)
-        back(1, 2, 1)
-        scatter(1, 2, 1)
         for c in range(NC):
-            middle(2, E, c, ("xs0", "xs1", "first")[c])
+            middle(1, 2, c, ("first", "twin", "y10")[c])
+            back(1, 2, c)
+            scatter(1, 2, c)
+        for c in range(NC):
+            middle(2, E, c, ("xs0", "xs1", "xs0b")[c])
             back(2, E, c)
             scatter(2, E, c)
         for c in range(NC):

@@ -16,8 +16,12 @@ ALU = mybir.AluOpType
 P = 128
 PACK = 4
 M, K, T, E, C, N = 512, 512, 512, 4, 128, 384
-NC = N // P
+CHUNKS = N // P
 FLOPS = 2 * M * K * T + 2 * K * N * T
+
+FIRST_PAIR_TOKENS = 336
+SECOND_PAIR_TOKENS = 144
+LATE_WU_GROUPS = 48
 
 
 def tile_moe_prv_lin_relu2_kernel(tc, uT, wu, w_words, w_scales, b, gate, offs, out):
@@ -27,13 +31,15 @@ def tile_moe_prv_lin_relu2_kernel(tc, uT, wu, w_words, w_scales, b, gate, offs, 
         psum = ctx.enter_context(tc.psum_pool(name="psum", bufs=1))
 
         offsets = keep.tile([P, E * C // 16], U16, name="offsets")
-        u_rows = uT.rearrange("(p j) t -> p j t", j=PACK)
+
         block = P * PACK
         later = T - C
-        early = 2 * (later + C)
-        stage = keep.tile([P, early + PACK * block], BF16, name="stage", align_bytes=64)
-        wu_grouped = stage[:, early:]
-        u_first = keep.tile([P, 2, T], F32, name="u_first", tag="u_raw0", align_bytes=64)
+        wu_start = 2 * (later + C)
+        stage = keep.tile([P, wu_start + PACK * block], BF16, name="stage", align_bytes=64)
+        wu_grouped = stage[:, wu_start:]
+
+        u_rows = uT.rearrange("(p j) t -> p j t", j=PACK)
+        u_first = keep.tile([P, 2, T], F32, name="u_first", tag="u_first", align_bytes=64)
         u_raw = [u_first[:], wu_grouped.bitcast(F32).rearrange("p (j t) -> p j t", j=2)]
         wu_rows = wu.rearrange("(p j) k -> p j k", j=PACK)
         reuse = ctx.enter_context(tc.tile_pool(name="reuse", bufs=1))
@@ -45,86 +51,86 @@ def tile_moe_prv_lin_relu2_kernel(tc, uT, wu, w_words, w_scales, b, gate, offs, 
         nc.sync.dma_start(offsets[:], offs)
         nc.sync.dma_start(u_raw[1], u_rows[:, 2:4, :])
         for h in range(2):
-            nc.sync.dma_start(wu_raw[h], wu_rows[:, :, h * (K // 2) : (h + 1) * (K // 2)])
-        bias = keep.tile([P, NC, E], F32, name="bias")
+            nc.sync.dma_start(wu_raw[h][:], wu_rows[:, :, h * (K // 2) : (h + 1) * (K // 2)])
+
+        bias = keep.tile([P, CHUNKS, E], F32, name="bias")
         nc.sync.dma_start(bias[:], b.rearrange("(c p) e -> p c e", p=P))
         gate_first = keep.tile([P, C], F32, name="gate_first")
         nc.sync.dma_start(gate_first[:], gate[:P, :C])
+
         w_plane = keep.tile([P, E * N], U8, name="w_plane", align_bytes=64)
         nc.gpsimd.memset(w_plane[:].bitcast(I32), 0)
-        for q in range(4):
+        for quadrant in range(4):
             nc.sync.dma_start(
-                w_plane[32 * q : 32 * q + 4, :].bitcast(I32).rearrange("r (e n) -> r e n", e=E),
-                w_scales[:, 0, 4 * q : 4 * q + 4, :].bitcast(I32).rearrange("e r n -> r e n"),
+                w_plane[32 * quadrant : 32 * quadrant + 4, :].bitcast(I32).rearrange("r (e n) -> r e n", e=E),
+                w_scales[:, 0, 4 * quadrant : 4 * quadrant + 4, :].bitcast(I32).rearrange("e r n -> r e n"),
             )
         w_codes = keep.tile([P, E * 2 * N], U8, name="w_codes", align_bytes=64)
         nc.sync.dma_start(
             w_codes[:].bitcast(I32).rearrange("p (e n) -> p e n", e=E),
             w_words[:, 0, :, :].bitcast(I32).rearrange("e p n -> p e n"),
         )
-        gate_rest = keep.tile([P, (E - 1) * C], F32, name="gate_rest")
+        gate_rest = keep.tile([P, later], F32, name="gate_rest")
         nc.sync.dma_start(gate_rest[:], gate[:P, C:])
 
-        def gates(c, e0, e1):
-            return gate_first[:] if e1 == 1 else gate_rest[:, (e0 - 1) * C : (e1 - 1) * C]
-
-        u_pairs = [keep.tile([P, T * 2], BF16, name=f"u_pairs{h}", tag=("pairs0", "u_raw0")[h], align_bytes=64) for h in range(2)]
-
-        def cast_u(h, share):
-            dst = u_pairs[h][:].rearrange("p (t j) -> p t j", j=2)
-            src = u_raw[h].rearrange("p j t -> p t j")
-            nc.vector.tensor_copy(dst[:, :share], src[:, :share])
-            nc.scalar.copy(dst[:, share:], src[:, share:])
+        def gates(e0, e1):
+            return gate_first[:] if e0 == 0 else gate_rest[:, (e0 - 1) * C : (e1 - 1) * C]
 
         def slot_offsets(e0, e1):
             return offsets[:, e0 * (C // 16) : e1 * (C // 16)]
 
+        u_pairs = [
+            keep.tile([P, T * 2], BF16, name="u_pairs0", align_bytes=64),
+            keep.tile([P, T * 2], BF16, name="u_pairs1", tag="u_first", align_bytes=64),
+        ]
+
+        def cast_u(h, vector_tokens):
+            dst = u_pairs[h][:].rearrange("p (t j) -> p t j", j=2)
+            src = u_raw[h].rearrange("p j t -> p t j")
+            nc.vector.tensor_copy(dst[:, :vector_tokens], src[:, :vector_tokens])
+            nc.scalar.copy(dst[:, vector_tokens:], src[:, vector_tokens:])
+
+        u_slots = {0: keep.tile([P, C * PACK], BF16, name="u_slots0", align_bytes=64)}
+
+        def gather_first(h):
+            words = u_slots[0][:].bitcast(U32).rearrange("p (s h) -> p s h", h=2)
+            nc.vector.tensor_copy(words[:, :, h], u_pairs[h][:].bitcast(U32).indirect(slot_offsets(0, 1)))
 
         def gather(h, e0, e1):
             row = stage[:, 2 * (h * later + (e0 - 1) * C) : 2 * (h * later + (e1 - 1) * C)]
             nc.vector.tensor_copy(row.bitcast(U32), u_pairs[h][:].bitcast(U32).indirect(slot_offsets(e0, e1)))
 
-        first_slots = keep.tile([P, C * PACK], BF16, name="first_slots", align_bytes=64)
-        u_slots = {0: first_slots[:]}
-
-        def gather_first(h):
-            words = first_slots[:].bitcast(U32).rearrange("p (s h) -> p s h", h=2)
-            nc.vector.tensor_copy(words[:, :, h], u_pairs[h][:].bitcast(U32).indirect(slot_offsets(0, 1)))
-
         def weave(copy, dtype, e0, e1, woven):
-            u_slots[e0] = woven[:]
+            u_slots[e0] = woven
             rows = stage[:, : 4 * later].bitcast(dtype).rearrange("p (h s) -> p s h", h=2)
-            copy(u_slots[e0].bitcast(dtype).rearrange("p (s h) -> p s h", h=2), rows[:, (e0 - 1) * C : (e1 - 1) * C, :])
+            copy(woven[:].bitcast(dtype).rearrange("p (s h) -> p s h", h=2), rows[:, (e0 - 1) * C : (e1 - 1) * C, :])
 
         u_quantised = {}
 
-        def quantise_u(e0, e1, u_codes):
-            if e0 == 0:
-                u_plane = keep.tile([P, C], U8, name="u_plane0", align_bytes=64)[:]
-            elif e0 == 1:
-                u_plane = keep.tile([P, C], U8, name="u_plane1", align_bytes=64)[:]
-            else:
-                u_plane = keep.tile([P, 2 * C], U8, name="u_plane2", align_bytes=64)[:]
-            nc.vector.quantize_mx(out=u_codes[:].bitcast(FP8X4), scales=u_plane, in_=u_slots[e0])
+        def quantise_u(e0, e1, codes_tag):
+            u_codes = keep.tile([P, (e1 - e0) * C], U32, name=f"u_codes{e0}", tag=codes_tag, align_bytes=64)
+            u_plane = keep.tile([P, (e1 - e0) * C], U8, name=f"u_plane{e0}", align_bytes=64)
+            nc.vector.quantize_mx(out=u_codes[:].bitcast(FP8X4), scales=u_plane[:], in_=u_slots[e0][:])
             for e in range(e0, e1):
                 cols = slice((e - e0) * C, (e - e0 + 1) * C)
                 u_quantised[e] = (u_codes[:, cols], u_plane[:, cols])
 
-        cast_u(0, 336)
+        cast_u(0, FIRST_PAIR_TOKENS)
         gather_first(0)
-        cast_u(1, 96)
+        cast_u(1, SECOND_PAIR_TOKENS)
         gather(0, 1, E)
         gather_first(1)
         gather(1, 1, 2)
-        quantise_u(0, 1, keep.tile([P, C], U32, name="u_codes0", align_bytes=64))
+        quantise_u(0, 1, "u_codes0")
 
-        wu_dst = wu_grouped.rearrange("p (t m j) -> p m j t", t=PACK, j=PACK)
         half = P // 2
+        split = half + LATE_WU_GROUPS
+        wu_dst = wu_grouped.rearrange("p (t m j) -> p m j t", t=PACK, j=PACK)
         wu_src = [wu_raw[h][:].rearrange("p j (m t) -> p m j t", t=PACK) for h in range(2)]
         nc.scalar.copy(wu_dst[:, :half], wu_src[0])
         for t in range(0, PACK, 2):
-            nc.vector.tensor_copy(wu_dst[:, half : half + 48, :, t : t + 2], wu_src[1][:, :48, :, t : t + 2])
-            nc.scalar.copy(wu_dst[:, half + 48 :, :, t : t + 2], wu_src[1][:, 48:, :, t : t + 2])
+            nc.vector.tensor_copy(wu_dst[:, half:split, :, t : t + 2], wu_src[1][:, :LATE_WU_GROUPS, :, t : t + 2])
+            nc.scalar.copy(wu_dst[:, split:, :, t : t + 2], wu_src[1][:, LATE_WU_GROUPS:, :, t : t + 2])
         wu_codes = keep.tile([P, K], U32, name="wu_codes", align_bytes=64)
         wu_plane = keep.tile([P, K], U8, name="wu_plane", align_bytes=64)
         for t in range(PACK):
@@ -133,9 +139,10 @@ def tile_moe_prv_lin_relu2_kernel(tc, uT, wu, w_words, w_scales, b, gate, offs, 
                 scales=wu_plane[:, t * P : (t + 1) * P],
                 in_=wu_grouped[:, t * block : (t + 1) * block],
             )
+
         weave(nc.scalar.copy, U32, 1, 2, reuse.tile([P, C * PACK], BF16, name="u_slots1", align_bytes=64, offset=0))
         gather(1, 2, E)
-        quantise_u(1, 2, keep.tile([P, C], U32, name="u_codes1", align_bytes=64))
+        quantise_u(1, 2, "u_codes1")
         weave(nc.vector.tensor_copy, I32, 2, E, keep.tile([P, 2 * C * PACK], BF16, name="u_slots2", align_bytes=64))
 
         x_quantised = {}
@@ -143,15 +150,16 @@ def tile_moe_prv_lin_relu2_kernel(tc, uT, wu, w_words, w_scales, b, gate, offs, 
         factors = {}
         outs = {}
 
-        def front(e0, e1):
-            x_grouped = keep.tile([P, (e1 - e0) * C * PACK], BF16, name=f"x_grouped{e0}", tag=f"xg{e0}", align_bytes=64)
+        def project(e0, e1, banks, x_plane):
+            x_grouped = keep.tile(
+                [P, (e1 - e0) * C * PACK], BF16, name=f"x_grouped{e0}", tag=f"x_grouped{e0}", align_bytes=64
+            )
             for e in range(e0, e1):
                 u_codes, u_plane = u_quantised[e]
-                part = x_grouped[:, (e - e0) * C * PACK : (e - e0 + 1) * C * PACK].rearrange("p (s t) -> p s t", t=PACK)
-                tags = (("xs0", "xs0b"), ("xs1",), ("first",), ("twin",))[e]
-                width = PACK // len(tags)
-                for i, tag in enumerate(tags):
-                    x_sums = psum.tile([P, width, C], F32, name=f"x_sums{e}{i}", tag=tag)
+                slots = x_grouped[:, (e - e0) * C * PACK : (e - e0 + 1) * C * PACK].rearrange("p (s t) -> p s t", t=PACK)
+                width = PACK // len(banks[e - e0])
+                for i, bank in enumerate(banks[e - e0]):
+                    x_sums = psum.tile([P, width, C], F32, name=f"x_sums{e}{i}", tag=bank)
                     for t in range(i * width, (i + 1) * width):
                         nc.tensor.matmul_mx(
                             out=x_sums[:, t - i * width, :],
@@ -162,12 +170,8 @@ def tile_moe_prv_lin_relu2_kernel(tc, uT, wu, w_words, w_scales, b, gate, offs, 
                             start=True,
                             stop=True,
                         )
-                    nc.scalar.copy(part[:, :, i * width : (i + 1) * width], x_sums[:].rearrange("p t s -> p s t"))
+                    nc.scalar.copy(slots[:, :, i * width : (i + 1) * width], x_sums[:].rearrange("p t s -> p s t"))
             x_codes = keep.tile([P, (e1 - e0) * C], U32, name=f"x_codes{e0}", align_bytes=64)
-            if e0 == 1:
-                x_plane = w_codes[:, :C]
-            else:
-                x_plane = keep.tile([P, (e1 - e0) * C], U8, name=f"x_plane{e0}", align_bytes=64)[:]
             nc.vector.quantize_mx(out=x_codes[:].bitcast(FP8X4), scales=x_plane, in_=x_grouped[:])
             for e in range(e0, e1):
                 cols = slice((e - e0) * C, (e - e0 + 1) * C)
@@ -186,57 +190,57 @@ def tile_moe_prv_lin_relu2_kernel(tc, uT, wu, w_words, w_scales, b, gate, offs, 
                 stop=True,
             )
 
-        def middle(e0, e1, c, tag):
-            bank = psum.tile([P, (e1 - e0) * C], F32, name=f"y_sums{e0}{c}", tag=tag)
+        def multiply(e0, e1, c, bank):
+            sums = psum.tile([P, (e1 - e0) * C], F32, name=f"y_sums{e0}{c}", tag=bank)
             for e in range(e0, e1):
-                y_sums[e, c] = bank[:, (e - e0) * C : (e - e0 + 1) * C]
+                y_sums[e, c] = sums[:, (e - e0) * C : (e - e0 + 1) * C]
                 expert_matmul(y_sums[e, c], e, c)
 
-        def twin_chunk():
-            twin = psum.tile([P, C], F32, name="y_twin", tag="twin")
-            expert_matmul(twin[:], 0, 0)
-            gated = keep.tile([P, C], F32, name="gated")
-            nc.vector.scalar_tensor_tensor(gated[:], twin[:], bias[:, 0, 0:1], gates(0, 0, 1), ALU.add, ALU.mult)
-            factors[0, 0] = [gated[:]]
-
-        def back(e0, e1, c):
+        def rectify(e0, e1, c):
             relu = keep.tile([P, (e1 - e0) * C], F32, name=f"relu{e0}{c}", align_bytes=64)
             for e in range(e0, e1):
                 nc.scalar.activation(
                     relu[:, (e - e0) * C : (e - e0 + 1) * C], y_sums[e, c], ACT.Relu, bias=bias[:, c, e : e + 1]
                 )
-            if (e0, c) in factors:
-                factors[e0, c].append(relu[:])
-            else:
-                squared = keep.tile([P, (e1 - e0) * C], F32, name=f"y{e0}{c}", align_bytes=64)
-                nc.scalar.activation(squared[:], relu[:], ACT.Square)
-                factors[e0, c] = [squared[:], gates(c, e0, e1)]
+            return relu
+
+        def epilogue(e0, e1, c):
+            relu = rectify(e0, e1, c)
+            squared = keep.tile([P, (e1 - e0) * C], F32, name=f"squared{e0}{c}", align_bytes=64)
+            nc.scalar.activation(squared[:], relu[:], ACT.Square)
+            factors[e0, c] = (squared[:], gates(e0, e1))
 
         def scatter(e0, e1, c):
             if c not in outs:
                 outs[c] = keep.tile([P, T], F32, name=f"out{c}", align_bytes=64)
             nc.vector.tensor_tensor(outs[c][:].indirect(slot_offsets(e0, e1)), *factors[e0, c], ALU.mult)
 
-        front(0, 1)
-        quantise_u(2, E, keep.tile([P, 2 * C], U32, name="u_codes2", tag="xg0", align_bytes=64))
-        middle(0, 1, 0, "first")
-        twin_chunk()
-        middle(0, 1, 1, "y01")
-        middle(0, 1, 2, "y02")
-        back(0, 1, 0)
-        front(1, 2)
+        project(0, 1, [("x0_low", "x0_high")], keep.tile([P, C], U8, name="x_plane0", align_bytes=64)[:])
+        quantise_u(2, E, "x_grouped0")
+
+        multiply(0, 1, 0, "first")
+        twin = psum.tile([P, C], F32, name="y_twin", tag="twin")
+        expert_matmul(twin[:], 0, 0)
+        gated = keep.tile([P, C], F32, name="gated")
+        nc.vector.scalar_tensor_tensor(gated[:], twin[:], bias[:, 0, 0:1], gates(0, 1), ALU.add, ALU.mult)
+        multiply(0, 1, 1, "y01")
+        multiply(0, 1, 2, "y02")
+        factors[0, 0] = (gated[:], rectify(0, 1, 0)[:])
+
+        project(1, 2, [("x1",)], w_codes[:, :C])
         scatter(0, 1, 0)
-        for c in range(1, NC):
-            back(0, 1, c)
+        for c in range(1, CHUNKS):
+            epilogue(0, 1, c)
             scatter(0, 1, c)
-        front(2, E)
-        for c in range(NC):
-            middle(1, 2, c, ("first", "twin", "y10")[c])
-            back(1, 2, c)
+
+        project(2, E, [("first",), ("twin",)], keep.tile([P, 2 * C], U8, name="x_plane2", align_bytes=64)[:])
+        for c, bank in enumerate(("y10", "twin", "first")):
+            multiply(1, 2, c, bank)
+            epilogue(1, 2, c)
             scatter(1, 2, c)
-        for c in range(NC):
-            middle(2, E, c, ("xs0", "xs1", "xs0b")[c])
-            back(2, E, c)
+        for c, bank in enumerate(("x0_low", "x1", "x0_high")):
+            multiply(2, E, c, bank)
+            epilogue(2, E, c)
             scatter(2, E, c)
-        for c in range(NC):
+        for c in range(CHUNKS):
             nc.sync.dma_start(out[c * P : (c + 1) * P, :], outs[c][:])

@@ -21,7 +21,8 @@ FLOPS = 2 * M * K * T + 2 * K * N * T
 
 FIRST_PAIR_TOKENS = 336
 SECOND_PAIR_TOKENS = 144
-LATE_WU_GROUPS = 48
+EARLY_WU_GROUPS = 16
+LATE_WU_GROUPS = 40
 
 
 def tile_moe_prv_lin_relu2_kernel(tc, uT, wu, w_words, w_scales, b, gate, offs, out):
@@ -59,7 +60,7 @@ def tile_moe_prv_lin_relu2_kernel(tc, uT, wu, w_words, w_scales, b, gate, offs, 
         nc.sync.dma_start(gate_first[:], gate[:P, :C])
 
         w_plane = keep.tile([P, E * N], U8, name="w_plane", align_bytes=64)
-        nc.gpsimd.memset(w_plane[:].bitcast(I32), 0)
+        nc.vector.memset(w_plane[:].bitcast(I32), 0)
         for quadrant in range(4):
             nc.sync.dma_start(
                 w_plane[32 * quadrant : 32 * quadrant + 4, :].bitcast(I32).rearrange("r (e n) -> r e n", e=E),
@@ -121,13 +122,14 @@ def tile_moe_prv_lin_relu2_kernel(tc, uT, wu, w_words, w_scales, b, gate, offs, 
         gather(0, 1, E)
         gather_first(1)
         gather(1, 1, 2)
-        quantise_u(0, 1, "u_codes0")
 
         half = P // 2
         split = half + LATE_WU_GROUPS
         wu_dst = wu_grouped.rearrange("p (t m j) -> p m j t", t=PACK, j=PACK)
         wu_src = [wu_raw[h][:].rearrange("p j (m t) -> p m j t", t=PACK) for h in range(2)]
-        nc.scalar.copy(wu_dst[:, :half], wu_src[0])
+        nc.vector.tensor_copy(wu_dst[:, :EARLY_WU_GROUPS], wu_src[0][:, :EARLY_WU_GROUPS])
+        nc.scalar.copy(wu_dst[:, EARLY_WU_GROUPS:half], wu_src[0][:, EARLY_WU_GROUPS:])
+        quantise_u(0, 1, "u_codes0")
         for t in range(0, PACK, 2):
             nc.vector.tensor_copy(wu_dst[:, half:split, :, t : t + 2], wu_src[1][:, :LATE_WU_GROUPS, :, t : t + 2])
             nc.scalar.copy(wu_dst[:, split:, :, t : t + 2], wu_src[1][:, LATE_WU_GROUPS:, :, t : t + 2])

@@ -56,8 +56,8 @@ def tile_moe_prv_lin_relu2_kernel(tc, uT, wu, w_words, w_scales, b, gate, offs, 
 
         bias = keep.tile([P, CHUNKS, E], F32, name="bias")
         nc.sync.dma_start(bias[:], b.rearrange("(c p) e -> p c e", p=P))
-        gate_first = keep.tile([P, C], F32, name="gate_first")
-        nc.sync.dma_start(gate_first[:], gate[:P, :C])
+        gate_rows = keep.tile([P, T], F32, name="gate_rows", align_bytes=64)
+        nc.sync.dma_start(gate_rows[:, :C], gate[:P, :C])
 
         w_plane = keep.tile([P, E * N], U8, name="w_plane", align_bytes=64)
         nc.vector.memset(w_plane[:].bitcast(I32), 0)
@@ -71,11 +71,10 @@ def tile_moe_prv_lin_relu2_kernel(tc, uT, wu, w_words, w_scales, b, gate, offs, 
             w_codes[:].bitcast(I32).rearrange("p (e n) -> p e n", e=E),
             w_words[:, 0, :, :].bitcast(I32).rearrange("e p n -> p e n"),
         )
-        gate_rest = keep.tile([P, later], F32, name="gate_rest")
-        nc.sync.dma_start(gate_rest[:], gate[:P, C:])
+        nc.sync.dma_start(gate_rows[:, C:], gate[:P, C:])
 
         def gates(e0, e1):
-            return gate_first[:] if e0 == 0 else gate_rest[:, (e0 - 1) * C : (e1 - 1) * C]
+            return gate_rows[:, e0 * C : e1 * C]
 
         def slot_offsets(e0, e1):
             return offsets[:, e0 * (C // 16) : e1 * (C // 16)]
@@ -217,6 +216,16 @@ def tile_moe_prv_lin_relu2_kernel(tc, uT, wu, w_words, w_scales, b, gate, offs, 
                 outs[c] = keep.tile([P, T], F32, name=f"out{c}", align_bytes=64)
             nc.vector.tensor_tensor(outs[c][:].indirect(slot_offsets(e0, e1)), *factors[e0, c], ALU.mult)
 
+        def finish(e0, e1, c):
+            product = keep.tile([P, (e1 - e0) * C], F32, name=f"product{e0}{c}", align_bytes=64)
+            nc.vector.tensor_tensor(product[:], *factors[e0, c], ALU.mult)
+            factors[e0, c] = product
+
+        def scatter_copy(e0, e1, c):
+            if c not in outs:
+                outs[c] = keep.tile([P, T], F32, name=f"out{c}", align_bytes=64)
+            nc.scalar.activation(outs[c][:].indirect(slot_offsets(e0, e1)), factors[e0, c][:], ACT.Copy)
+
         project(0, 1, [("x0_low", "x0_high")], keep.tile([P, C], U8, name="x_plane0", align_bytes=64)[:])
         quantise_u(2, E, "x_grouped0")
 
@@ -226,23 +235,31 @@ def tile_moe_prv_lin_relu2_kernel(tc, uT, wu, w_words, w_scales, b, gate, offs, 
         gated = keep.tile([P, C], F32, name="gated")
         nc.vector.scalar_tensor_tensor(gated[:], twin[:], bias[:, 0, 0:1], gates(0, 1), ALU.add, ALU.mult)
         multiply(0, 1, 1, "y01")
-        multiply(0, 1, 2, "y02")
         factors[0, 0] = (gated[:], rectify(0, 1, 0)[:])
 
         project(1, 2, [("x1",)], w_codes[:, :C])
         scatter(0, 1, 0)
-        for c in range(1, CHUNKS):
-            epilogue(0, 1, c)
-            scatter(0, 1, c)
+        epilogue(0, 1, 1)
+        scatter(0, 1, 1)
 
         project(2, E, [("first",), ("twin",)], keep.tile([P, 2 * C], U8, name="x_plane2", align_bytes=64)[:])
-        for c, bank in enumerate(("y10", "twin", "first")):
+        for c, bank in enumerate(("y10", "twin")):
             multiply(1, 2, c, bank)
             epilogue(1, 2, c)
             scatter(1, 2, c)
-        for c, bank in enumerate(("x0_low", "x1", "x0_high")):
-            multiply(2, E, c, bank)
-            epilogue(2, E, c)
-            scatter(2, E, c)
+        multiply(0, 2, 2, "first")
+        epilogue(0, 2, 2)
+        finish(0, 2, 2)
+        multiply(2, E, 0, "x0_low")
+        epilogue(2, E, 0)
+        scatter(2, E, 0)
+        multiply(2, E, 2, "x0_high")
+        epilogue(2, E, 2)
+        finish(2, E, 2)
+        multiply(2, E, 1, "x1")
+        epilogue(2, E, 1)
+        scatter(2, E, 1)
+        scatter_copy(0, 2, 2)
+        scatter_copy(2, E, 2)
         for c in range(CHUNKS):
             nc.sync.dma_start(out[c * P : (c + 1) * P, :], outs[c][:])

@@ -142,9 +142,8 @@ def tile_moe_prv_lin_relu2_kernel(tc, uT, wu, w_words, w_scales, b, gate, offs, 
             )
 
         weave(nc.scalar.copy, U32, 1, 2, reuse.tile([P, C * PACK], BF16, name="u_slots1", align_bytes=64, offset=0))
-        gather(1, 2, E)
         quantise_u(1, 2, "u_codes1")
-        weave(nc.vector.tensor_copy, I32, 2, E, keep.tile([P, 2 * C * PACK], BF16, name="u_slots2", align_bytes=64))
+        gather(1, 2, E)
 
         x_quantised = {}
         y_sums = {}
@@ -198,7 +197,8 @@ def tile_moe_prv_lin_relu2_kernel(tc, uT, wu, w_words, w_scales, b, gate, offs, 
                 expert_matmul(y_sums[e, c], e, c)
 
         def rectify(e0, e1, c):
-            relu = keep.tile([P, (e1 - e0) * C], F32, name=f"relu{e0}{c}", align_bytes=64)
+            tag = "x_grouped2" if (e0, c) == (0, 1) else f"relu{e0}{c}"
+            relu = keep.tile([P, (e1 - e0) * C], F32, name=f"relu{e0}{c}", tag=tag, align_bytes=64)
             for e in range(e0, e1):
                 nc.scalar.activation(
                     relu[:, (e - e0) * C : (e - e0 + 1) * C], y_sums[e, c], ACT.Relu, bias=bias[:, c, e : e + 1]
@@ -211,23 +211,28 @@ def tile_moe_prv_lin_relu2_kernel(tc, uT, wu, w_words, w_scales, b, gate, offs, 
             nc.scalar.activation(squared[:], relu[:], ACT.Square)
             factors[e0, c] = (squared[:], gates(e0, e1))
 
+        def window(c):
+            if c not in outs:
+                tag = "x_grouped2" if c == CHUNKS - 1 else f"out{c}"
+                outs[c] = keep.tile([P, T], F32, name=f"out{c}", tag=tag, align_bytes=64)
+            return outs[c]
+
         def scatter(e0, e1, c):
-            if c not in outs:
-                outs[c] = keep.tile([P, T], F32, name=f"out{c}", align_bytes=64)
-            nc.vector.tensor_tensor(outs[c][:].indirect(slot_offsets(e0, e1)), *factors[e0, c], ALU.mult)
+            nc.vector.tensor_tensor(window(c)[:].indirect(slot_offsets(e0, e1)), *factors[e0, c], ALU.mult)
 
-        def finish(e0, e1, c):
-            product = keep.tile([P, (e1 - e0) * C], F32, name=f"product{e0}{c}", align_bytes=64)
-            nc.vector.tensor_tensor(product[:], *factors[e0, c], ALU.mult)
-            factors[e0, c] = product
-
-        def scatter_copy(e0, e1, c):
-            if c not in outs:
-                outs[c] = keep.tile([P, T], F32, name=f"out{c}", align_bytes=64)
-            nc.scalar.activation(outs[c][:].indirect(slot_offsets(e0, e1)), factors[e0, c][:], ACT.Copy)
+        def scatter_copy(e0, e1, c, product):
+            nc.scalar.activation(window(c)[:].indirect(slot_offsets(e0, e1)), product, ACT.Copy)
 
         project(0, 1, [("x0_low", "x0_high")], keep.tile([P, C], U8, name="x_plane0", align_bytes=64)[:])
-        quantise_u(2, E, "x_grouped0")
+        weave(
+            nc.vector.tensor_copy,
+            I32,
+            2,
+            E,
+            keep.tile([P, 2 * C * PACK], BF16, name="u_slots2", tag="x_grouped0", align_bytes=64),
+        )
+        project(1, 2, [("x1",)], keep.tile([P, C], U8, name="x_plane1", align_bytes=64)[:])
+        quantise_u(2, E, "u_codes2")
 
         multiply(0, 1, 0, "first")
         twin = psum.tile([P, C], F32, name="y_twin", tag="twin")
@@ -235,31 +240,44 @@ def tile_moe_prv_lin_relu2_kernel(tc, uT, wu, w_words, w_scales, b, gate, offs, 
         gated = keep.tile([P, C], F32, name="gated")
         nc.vector.scalar_tensor_tensor(gated[:], twin[:], bias[:, 0, 0:1], gates(0, 1), ALU.add, ALU.mult)
         multiply(0, 1, 1, "y01")
+        multiply(0, 1, 2, "y02")
         factors[0, 0] = (gated[:], rectify(0, 1, 0)[:])
 
-        project(1, 2, [("x1",)], w_codes[:, :C])
         scatter(0, 1, 0)
         epilogue(0, 1, 1)
         scatter(0, 1, 1)
+        epilogue(0, 1, 2)
 
         project(2, E, [("first",), ("twin",)], keep.tile([P, 2 * C], U8, name="x_plane2", align_bytes=64)[:])
-        for c, bank in enumerate(("y10", "twin")):
-            multiply(1, 2, c, bank)
-            epilogue(1, 2, c)
-            scatter(1, 2, c)
-        multiply(0, 2, 2, "first")
-        epilogue(0, 2, 2)
-        finish(0, 2, 2)
+        scatter(0, 1, 2)
+        multiply(1, 2, 0, "twin")
+        epilogue(1, 2, 0)
+        scatter(1, 2, 0)
+
+        late_sums = psum.tile([P, 2, C], F32, name="late_sums", tag="first")
+        late_relu = keep.tile([P, 2, C], F32, name="late_relu", align_bytes=64)
+        late_squared = keep.tile([P, 2, C], F32, name="late_squared", align_bytes=64)
+        products = keep.tile([P, E * C], F32, name="products", tag="u_codes2", align_bytes=64)
+        late_product = products[:, : 2 * C].rearrange("p (c s) -> p c s", c=2)
+        for c in (1, 2):
+            expert_matmul(late_sums[:, c - 1, :], 1, c)
+        for c in (1, 2):
+            nc.scalar.activation(late_relu[:, c - 1, :], late_sums[:, c - 1, :], ACT.Relu, bias=bias[:, c, 1:2])
+        nc.scalar.activation(late_squared[:], late_relu[:], ACT.Square)
+        nc.vector.tensor_tensor(
+            late_product, late_squared[:], gates(1, 2).unsqueeze(1).to_broadcast([P, 2, C]), ALU.mult
+        )
+
+        multiply(2, E, 2, "x0_high")
+        epilogue(2, E, 2)
+        nc.vector.tensor_tensor(products[:, 2 * C :], *factors[2, 2], ALU.mult)
         multiply(2, E, 0, "x0_low")
         epilogue(2, E, 0)
         scatter(2, E, 0)
-        multiply(2, E, 2, "x0_high")
-        epilogue(2, E, 2)
-        finish(2, E, 2)
         multiply(2, E, 1, "x1")
         epilogue(2, E, 1)
+        scatter_copy(1, 2, 1, products[:, :C])
         scatter(2, E, 1)
-        scatter_copy(0, 2, 2)
-        scatter_copy(2, E, 2)
+        scatter_copy(1, E, 2, products[:, C:])
         for c in range(CHUNKS):
             nc.sync.dma_start(out[c * P : (c + 1) * P, :], outs[c][:])

@@ -23,6 +23,7 @@ FIRST_PAIR_TOKENS = 336
 SECOND_PAIR_TOKENS = 144
 EARLY_WU_GROUPS = 16
 LATE_WU_GROUPS = 40
+LAST_CHUNK_SLOTS = 96
 
 
 def tile_moe_prv_lin_relu2_kernel(tc, uT, wu, w_words, w_scales, b, gate, offs, out):
@@ -257,7 +258,7 @@ def tile_moe_prv_lin_relu2_kernel(tc, uT, wu, w_words, w_scales, b, gate, offs, 
         late_sums = psum.tile([P, 2, C], F32, name="late_sums", tag="first")
         late_relu = keep.tile([P, 2, C], F32, name="late_relu", align_bytes=64)
         late_squared = keep.tile([P, 2, C], F32, name="late_squared", align_bytes=64)
-        products = keep.tile([P, E * C], F32, name="products", tag="u_codes2", align_bytes=64)
+        products = keep.tile([P, T - LAST_CHUNK_SLOTS], F32, name="products", tag="u_codes2", align_bytes=64)
         late_product = products[:, : 2 * C].rearrange("p (c s) -> p c s", c=2)
         for c in (1, 2):
             expert_matmul(late_sums[:, c - 1, :], 1, c)
@@ -270,7 +271,13 @@ def tile_moe_prv_lin_relu2_kernel(tc, uT, wu, w_words, w_scales, b, gate, offs, 
 
         multiply(2, E, 2, "x0_high")
         epilogue(2, E, 2)
-        nc.vector.tensor_tensor(products[:, 2 * C :], *factors[2, 2], ALU.mult)
+        shared = T - LAST_CHUNK_SLOTS
+        squared, gates_late = factors[2, 2]
+        kept = shared - 2 * C
+        nc.vector.tensor_tensor(products[:, 2 * C : shared], squared[:, :kept], gates_late[:, :kept], ALU.mult)
+        nc.vector.tensor_tensor(
+            window(2)[:].indirect(offsets[:, shared // 16 :]), squared[:, kept:], gates_late[:, kept:], ALU.mult
+        )
         multiply(2, E, 0, "x0_low")
         epilogue(2, E, 0)
         scatter(2, E, 0)
@@ -278,6 +285,6 @@ def tile_moe_prv_lin_relu2_kernel(tc, uT, wu, w_words, w_scales, b, gate, offs, 
         epilogue(2, E, 1)
         scatter_copy(1, 2, 1, products[:, :C])
         scatter(2, E, 1)
-        scatter_copy(1, E, 2, products[:, C:])
-        for c in range(CHUNKS):
+        nc.scalar.activation(window(2)[:].indirect(offsets[:, C // 16 : shared // 16]), products[:, C:], ACT.Copy)
+        for c in (0, 2, 1):
             nc.sync.dma_start(out[c * P : (c + 1) * P, :], outs[c][:])

@@ -23,6 +23,7 @@ FIRST_PAIR_TOKENS = 336
 SECOND_PAIR_TOKENS = 144
 EARLY_WU_GROUPS = 16
 LATE_WU_GROUPS = 40
+
 LAST_CHUNK_SLOTS = 96
 
 
@@ -108,8 +109,8 @@ def tile_moe_prv_lin_relu2_kernel(tc, uT, wu, w_words, w_scales, b, gate, offs, 
 
         u_quantised = {}
 
-        def quantise_u(e0, e1, codes_tag):
-            u_codes = keep.tile([P, (e1 - e0) * C], U32, name=f"u_codes{e0}", tag=codes_tag, align_bytes=64)
+        def quantise_u(e0, e1):
+            u_codes = keep.tile([P, (e1 - e0) * C], U32, name=f"u_codes{e0}", tag=f"u_codes{e0}", align_bytes=64)
             u_plane = keep.tile([P, (e1 - e0) * C], U8, name=f"u_plane{e0}", align_bytes=64)
             nc.vector.quantize_mx(out=u_codes[:].bitcast(FP8X4), scales=u_plane[:], in_=u_slots[e0][:])
             for e in range(e0, e1):
@@ -129,7 +130,7 @@ def tile_moe_prv_lin_relu2_kernel(tc, uT, wu, w_words, w_scales, b, gate, offs, 
         wu_src = [wu_raw[h][:].rearrange("p j (m t) -> p m j t", t=PACK) for h in range(2)]
         nc.vector.tensor_copy(wu_dst[:, :EARLY_WU_GROUPS], wu_src[0][:, :EARLY_WU_GROUPS])
         nc.scalar.copy(wu_dst[:, EARLY_WU_GROUPS:half], wu_src[0][:, EARLY_WU_GROUPS:])
-        quantise_u(0, 1, "u_codes0")
+        quantise_u(0, 1)
         for t in range(0, PACK, 2):
             nc.vector.tensor_copy(wu_dst[:, half:split, :, t : t + 2], wu_src[1][:, :LATE_WU_GROUPS, :, t : t + 2])
             nc.scalar.copy(wu_dst[:, split:, :, t : t + 2], wu_src[1][:, LATE_WU_GROUPS:, :, t : t + 2])
@@ -143,15 +144,14 @@ def tile_moe_prv_lin_relu2_kernel(tc, uT, wu, w_words, w_scales, b, gate, offs, 
             )
 
         weave(nc.scalar.copy, U32, 1, 2, reuse.tile([P, C * PACK], BF16, name="u_slots1", align_bytes=64, offset=0))
-        quantise_u(1, 2, "u_codes1")
+        quantise_u(1, 2)
         gather(1, 2, E)
 
         x_quantised = {}
         y_sums = {}
-        factors = {}
         outs = {}
 
-        def project(e0, e1, banks, x_plane):
+        def project(e0, e1, banks):
             x_grouped = keep.tile(
                 [P, (e1 - e0) * C * PACK], BF16, name=f"x_grouped{e0}", tag=f"x_grouped{e0}", align_bytes=64
             )
@@ -172,6 +172,9 @@ def tile_moe_prv_lin_relu2_kernel(tc, uT, wu, w_words, w_scales, b, gate, offs, 
                             stop=True,
                         )
                     nc.scalar.copy(slots[:, :, i * width : (i + 1) * width], x_sums[:].rearrange("p t s -> p s t"))
+            return x_grouped
+
+        def quantise_x(e0, e1, x_grouped, x_plane):
             x_codes = keep.tile([P, (e1 - e0) * C], U32, name=f"x_codes{e0}", align_bytes=64)
             nc.vector.quantize_mx(out=x_codes[:].bitcast(FP8X4), scales=x_plane, in_=x_grouped[:])
             for e in range(e0, e1):
@@ -197,8 +200,7 @@ def tile_moe_prv_lin_relu2_kernel(tc, uT, wu, w_words, w_scales, b, gate, offs, 
                 y_sums[e, c] = sums[:, (e - e0) * C : (e - e0 + 1) * C]
                 expert_matmul(y_sums[e, c], e, c)
 
-        def rectify(e0, e1, c):
-            tag = "x_grouped2" if (e0, c) == (0, 1) else f"relu{e0}{c}"
+        def rectify(e0, e1, c, tag):
             relu = keep.tile([P, (e1 - e0) * C], F32, name=f"relu{e0}{c}", tag=tag, align_bytes=64)
             for e in range(e0, e1):
                 nc.scalar.activation(
@@ -206,85 +208,84 @@ def tile_moe_prv_lin_relu2_kernel(tc, uT, wu, w_words, w_scales, b, gate, offs, 
                 )
             return relu
 
-        def epilogue(e0, e1, c):
-            relu = rectify(e0, e1, c)
+        def epilogue(e0, e1, c, relu_tag=None):
+            relu = rectify(e0, e1, c, relu_tag or f"relu{e0}{c}")
             squared = keep.tile([P, (e1 - e0) * C], F32, name=f"squared{e0}{c}", align_bytes=64)
             nc.scalar.activation(squared[:], relu[:], ACT.Square)
-            factors[e0, c] = (squared[:], gates(e0, e1))
+            return squared[:], gates(e0, e1)
 
-        def window(c):
+        def window(c, s0, s1):
             if c not in outs:
                 tag = "x_grouped2" if c == CHUNKS - 1 else f"out{c}"
                 outs[c] = keep.tile([P, T], F32, name=f"out{c}", tag=tag, align_bytes=64)
-            return outs[c]
+            return outs[c][:].indirect(offsets[:, s0 // 16 : s1 // 16])
 
-        def scatter(e0, e1, c):
-            nc.vector.tensor_tensor(window(c)[:].indirect(slot_offsets(e0, e1)), *factors[e0, c], ALU.mult)
+        def scatter_product(c, s0, s1, factor, other):
+            nc.vector.tensor_tensor(window(c, s0, s1), factor, other, ALU.mult)
 
-        def scatter_copy(e0, e1, c, product):
-            nc.scalar.activation(window(c)[:].indirect(slot_offsets(e0, e1)), product, ACT.Copy)
+        def scatter_copy(c, s0, s1, product):
+            nc.scalar.activation(window(c, s0, s1), product, ACT.Copy)
 
-        project(0, 1, [("x0_low", "x0_high")], keep.tile([P, C], U8, name="x_plane0", align_bytes=64)[:])
+        x_first = project(0, 1, [("x0_low", "x0_high")])
+        quantise_x(0, 1, x_first, keep.tile([P, C], U8, name="x_plane0", align_bytes=64)[:])
+        x_second = project(1, 2, [("x1",)])
         weave(
             nc.vector.tensor_copy,
             I32,
             2,
             E,
-            keep.tile([P, 2 * C * PACK], BF16, name="u_slots2", tag="x_grouped0", align_bytes=64),
+            keep.tile([P, 2 * C * PACK], BF16, name="u_slots2", tag="u_codes1", align_bytes=64),
         )
-        project(1, 2, [("x1",)], keep.tile([P, C], U8, name="x_plane1", align_bytes=64)[:])
-        quantise_u(2, E, "u_codes2")
+        quantise_u(2, E)
 
         multiply(0, 1, 0, "first")
         twin = psum.tile([P, C], F32, name="y_twin", tag="twin")
         expert_matmul(twin[:], 0, 0)
         gated = keep.tile([P, C], F32, name="gated")
         nc.vector.scalar_tensor_tensor(gated[:], twin[:], bias[:, 0, 0:1], gates(0, 1), ALU.add, ALU.mult)
+        quantise_x(1, 2, x_second, w_codes[:, :C])
         multiply(0, 1, 1, "y01")
         multiply(0, 1, 2, "y02")
-        factors[0, 0] = (gated[:], rectify(0, 1, 0)[:])
+        scatter_product(0, 0, C, gated[:], rectify(0, 1, 0, "relu00")[:])
+        scatter_product(1, 0, C, *epilogue(0, 1, 1, relu_tag="x_grouped2"))
+        last_of_first = epilogue(0, 1, 2)
 
-        scatter(0, 1, 0)
-        epilogue(0, 1, 1)
-        scatter(0, 1, 1)
-        epilogue(0, 1, 2)
-
-        project(2, E, [("first",), ("twin",)], keep.tile([P, 2 * C], U8, name="x_plane2", align_bytes=64)[:])
-        scatter(0, 1, 2)
+        x_late = project(2, E, [("first",), ("twin",)])
+        quantise_x(2, E, x_late, keep.tile([P, 2 * C], U8, name="x_plane2", align_bytes=64)[:])
+        scatter_product(2, 0, C, *last_of_first)
         multiply(1, 2, 0, "twin")
-        epilogue(1, 2, 0)
-        scatter(1, 2, 0)
+        scatter_product(0, C, 2 * C, *epilogue(1, 2, 0))
 
-        late_sums = psum.tile([P, 2, C], F32, name="late_sums", tag="first")
-        late_relu = keep.tile([P, 2, C], F32, name="late_relu", align_bytes=64)
-        late_squared = keep.tile([P, 2, C], F32, name="late_squared", align_bytes=64)
-        products = keep.tile([P, T - LAST_CHUNK_SLOTS], F32, name="products", tag="u_codes2", align_bytes=64)
-        late_product = products[:, : 2 * C].rearrange("p (c s) -> p c s", c=2)
+        handover = T - LAST_CHUNK_SLOTS
+        products = keep.tile([P, handover], F32, name="products", tag="u_codes2", align_bytes=64)
+
+        pair_sums = psum.tile([P, 2, C], F32, name="pair_sums", tag="first")
+        pair_relu = keep.tile([P, 2, C], F32, name="pair_relu", align_bytes=64)
+        pair_squared = keep.tile([P, 2, C], F32, name="pair_squared", align_bytes=64)
         for c in (1, 2):
-            expert_matmul(late_sums[:, c - 1, :], 1, c)
+            expert_matmul(pair_sums[:, c - 1, :], 1, c)
         for c in (1, 2):
-            nc.scalar.activation(late_relu[:, c - 1, :], late_sums[:, c - 1, :], ACT.Relu, bias=bias[:, c, 1:2])
-        nc.scalar.activation(late_squared[:], late_relu[:], ACT.Square)
+            nc.scalar.activation(pair_relu[:, c - 1, :], pair_sums[:, c - 1, :], ACT.Relu, bias=bias[:, c, 1:2])
+        nc.scalar.activation(pair_squared[:], pair_relu[:], ACT.Square)
         nc.vector.tensor_tensor(
-            late_product, late_squared[:], gates(1, 2).unsqueeze(1).to_broadcast([P, 2, C]), ALU.mult
+            products[:, : 2 * C].rearrange("p (c s) -> p c s", c=2),
+            pair_squared[:],
+            gates(1, 2).unsqueeze(1).to_broadcast([P, 2, C]),
+            ALU.mult,
         )
 
         multiply(2, E, 2, "x0_high")
-        epilogue(2, E, 2)
-        shared = T - LAST_CHUNK_SLOTS
-        squared, gates_late = factors[2, 2]
-        kept = shared - 2 * C
-        nc.vector.tensor_tensor(products[:, 2 * C : shared], squared[:, :kept], gates_late[:, :kept], ALU.mult)
-        nc.vector.tensor_tensor(
-            window(2)[:].indirect(offsets[:, shared // 16 :]), squared[:, kept:], gates_late[:, kept:], ALU.mult
-        )
+        squared, gate_late = epilogue(2, E, 2)
+        kept = handover - 2 * C
+        nc.vector.tensor_tensor(products[:, 2 * C :], squared[:, :kept], gate_late[:, :kept], ALU.mult)
+        scatter_product(2, handover, T, squared[:, kept:], gate_late[:, kept:])
         multiply(2, E, 0, "x0_low")
-        epilogue(2, E, 0)
-        scatter(2, E, 0)
+        scatter_product(0, 2 * C, T, *epilogue(2, E, 0))
         multiply(2, E, 1, "x1")
-        epilogue(2, E, 1)
-        scatter_copy(1, 2, 1, products[:, :C])
-        scatter(2, E, 1)
-        nc.scalar.activation(window(2)[:].indirect(offsets[:, C // 16 : shared // 16]), products[:, C:], ACT.Copy)
+        middle_of_late = epilogue(2, E, 1)
+        scatter_copy(1, C, 2 * C, products[:, :C])
+        scatter_product(1, 2 * C, T, *middle_of_late)
+        scatter_copy(2, C, handover, products[:, C:])
+
         for c in (0, 2, 1):
             nc.sync.dma_start(out[c * P : (c + 1) * P, :], outs[c][:])

@@ -24,6 +24,8 @@ SECOND_PAIR_TOKENS = 144
 EARLY_WU_GROUPS = 16
 LATE_WU_GROUPS = 40
 
+WARM_PASSES = 6
+WARM_COLUMNS = 32
 LAST_CHUNK_SLOTS = 96
 
 
@@ -131,6 +133,18 @@ def tile_moe_prv_lin_relu2_kernel(tc, uT, wu, w_words, w_scales, b, gate, offs, 
         nc.vector.tensor_copy(wu_dst[:, :EARLY_WU_GROUPS], wu_src[0][:, :EARLY_WU_GROUPS])
         nc.scalar.copy(wu_dst[:, EARLY_WU_GROUPS:half], wu_src[0][:, EARLY_WU_GROUPS:])
         quantise_u(0, 1)
+        unread = psum.tile([WARM_COLUMNS, C], F32, name="unread", tag="unread")
+        first_codes, first_plane = u_quantised[0]
+        for i in range(WARM_PASSES):
+            nc.tensor.matmul_mx(
+                out=unread[:],
+                lhsT=first_codes[:, :WARM_COLUMNS].bitcast(FP8X4),
+                lhsT_scale=first_plane[:, :WARM_COLUMNS],
+                rhs=first_codes.bitcast(FP8X4),
+                rhs_scale=first_plane,
+                start=True,
+                stop=True,
+            )
         for t in range(0, PACK, 2):
             nc.vector.tensor_copy(wu_dst[:, half:split, :, t : t + 2], wu_src[1][:, :LATE_WU_GROUPS, :, t : t + 2])
             nc.scalar.copy(wu_dst[:, split:, :, t : t + 2], wu_src[1][:, LATE_WU_GROUPS:, :, t : t + 2])

@@ -20,13 +20,11 @@ CHUNKS = N // P
 FLOPS = 2 * M * K * T + 2 * K * N * T
 
 FIRST_PAIR_TOKENS = 336
-SECOND_PAIR_TOKENS = 144
 EARLY_WU_GROUPS = 16
 LATE_WU_GROUPS = 40
-
 WARM_PASSES = 6
 WARM_COLUMNS = 32
-LAST_CHUNK_SLOTS = 96
+LAST_CHUNK_SLOTS = 64
 
 
 def tile_moe_prv_lin_relu2_kernel(tc, uT, wu, w_words, w_scales, b, gate, offs, out):
@@ -39,7 +37,7 @@ def tile_moe_prv_lin_relu2_kernel(tc, uT, wu, w_words, w_scales, b, gate, offs, 
 
         block = P * PACK
         later = T - C
-        wu_start = 2 * (later + C)
+        wu_start = 4 * later
         stage = keep.tile([P, wu_start + PACK * block], BF16, name="stage", align_bytes=64)
         wu_grouped = stage[:, wu_start:]
 
@@ -54,14 +52,15 @@ def tile_moe_prv_lin_relu2_kernel(tc, uT, wu, w_words, w_scales, b, gate, offs, 
         ]
         nc.sync.dma_start(u_raw[0], u_rows[:, 0:2, :])
         nc.sync.dma_start(offsets[:], offs)
-        nc.sync.dma_start(u_raw[1], u_rows[:, 2:4, :])
+        for tokens in (slice(0, T // 2), slice(T // 2, T)):
+            nc.sync.dma_start(u_raw[1][:, :, tokens], u_rows[:, 2:4, tokens])
         for h in range(2):
             nc.sync.dma_start(wu_raw[h][:], wu_rows[:, :, h * (K // 2) : (h + 1) * (K // 2)])
 
         bias = keep.tile([P, CHUNKS, E], F32, name="bias")
         nc.sync.dma_start(bias[:], b.rearrange("(c p) e -> p c e", p=P))
         gate_rows = keep.tile([P, T], F32, name="gate_rows", align_bytes=64)
-        nc.sync.dma_start(gate_rows[:, :C], gate[:P, :C])
+        nc.sync.dma_start(gate_rows[:], gate[:P, :])
 
         w_plane = keep.tile([P, E * N], U8, name="w_plane", align_bytes=64)
         nc.vector.memset(w_plane[:].bitcast(I32), 0)
@@ -75,34 +74,30 @@ def tile_moe_prv_lin_relu2_kernel(tc, uT, wu, w_words, w_scales, b, gate, offs, 
             w_codes[:].bitcast(I32).rearrange("p (e n) -> p e n", e=E),
             w_words[:, 0, :, :].bitcast(I32).rearrange("e p n -> p e n"),
         )
-        nc.sync.dma_start(gate_rows[:, C:], gate[:P, C:])
 
-        def gates(e0, e1):
-            return gate_rows[:, e0 * C : e1 * C]
-
-        def slot_offsets(e0, e1):
-            return offsets[:, e0 * (C // 16) : e1 * (C // 16)]
+        def slot_offsets(s0, s1):
+            return offsets[:, s0 // 16 : s1 // 16]
 
         u_pairs = [
             keep.tile([P, T * 2], BF16, name="u_pairs0", align_bytes=64),
             keep.tile([P, T * 2], BF16, name="u_pairs1", tag="u_first", align_bytes=64),
         ]
 
-        def cast_u(h, vector_tokens):
+        def cast_u(h, copy, tokens):
             dst = u_pairs[h][:].rearrange("p (t j) -> p t j", j=2)
             src = u_raw[h].rearrange("p j t -> p t j")
-            nc.vector.tensor_copy(dst[:, :vector_tokens], src[:, :vector_tokens])
-            nc.scalar.copy(dst[:, vector_tokens:], src[:, vector_tokens:])
+            for engine_copy, t0, t1 in zip(copy, tokens, tokens[1:]):
+                engine_copy(dst[:, t0:t1], src[:, t0:t1])
 
         u_slots = {0: keep.tile([P, C * PACK], BF16, name="u_slots0", align_bytes=64)}
 
         def gather_first(h):
             words = u_slots[0][:].bitcast(U32).rearrange("p (s h) -> p s h", h=2)
-            nc.vector.tensor_copy(words[:, :, h], u_pairs[h][:].bitcast(U32).indirect(slot_offsets(0, 1)))
+            nc.vector.tensor_copy(words[:, :, h], u_pairs[h][:].bitcast(U32).indirect(slot_offsets(0, C)))
 
         def gather(h, e0, e1):
             row = stage[:, 2 * (h * later + (e0 - 1) * C) : 2 * (h * later + (e1 - 1) * C)]
-            nc.vector.tensor_copy(row.bitcast(U32), u_pairs[h][:].bitcast(U32).indirect(slot_offsets(e0, e1)))
+            nc.vector.tensor_copy(row.bitcast(U32), u_pairs[h][:].bitcast(U32).indirect(slot_offsets(e0 * C, e1 * C)))
 
         def weave(copy, dtype, e0, e1, woven):
             u_slots[e0] = woven
@@ -111,29 +106,32 @@ def tile_moe_prv_lin_relu2_kernel(tc, uT, wu, w_words, w_scales, b, gate, offs, 
 
         u_quantised = {}
 
-        def quantise_u(e0, e1):
-            u_codes = keep.tile([P, (e1 - e0) * C], U32, name=f"u_codes{e0}", tag=f"u_codes{e0}", align_bytes=64)
+        def quantise_u(e0, e1, tag):
+            u_codes = keep.tile([P, (e1 - e0) * C], U32, name=f"u_codes{e0}", tag=tag, align_bytes=64)
             u_plane = keep.tile([P, (e1 - e0) * C], U8, name=f"u_plane{e0}", align_bytes=64)
             nc.vector.quantize_mx(out=u_codes[:].bitcast(FP8X4), scales=u_plane[:], in_=u_slots[e0][:])
             for e in range(e0, e1):
                 cols = slice((e - e0) * C, (e - e0 + 1) * C)
                 u_quantised[e] = (u_codes[:, cols], u_plane[:, cols])
 
-        cast_u(0, FIRST_PAIR_TOKENS)
+        cast_u(0, (nc.vector.tensor_copy, nc.scalar.copy), (0, FIRST_PAIR_TOKENS, T))
         gather_first(0)
-        cast_u(1, SECOND_PAIR_TOKENS)
         gather(0, 1, E)
+        cast_u(1, (nc.scalar.copy, nc.scalar.copy, nc.gpsimd.tensor_copy), (0, T // 2, 3 * T // 4, T))
         gather_first(1)
-        gather(1, 1, 2)
+        gather(1, 1, E)
+        quantise_u(0, 1, "u_codes0")
 
         half = P // 2
         split = half + LATE_WU_GROUPS
         wu_dst = wu_grouped.rearrange("p (t m j) -> p m j t", t=PACK, j=PACK)
         wu_src = [wu_raw[h][:].rearrange("p j (m t) -> p m j t", t=PACK) for h in range(2)]
-        nc.vector.tensor_copy(wu_dst[:, :EARLY_WU_GROUPS], wu_src[0][:, :EARLY_WU_GROUPS])
+        nc.gpsimd.tensor_copy(
+            wu_dst[:, :EARLY_WU_GROUPS].rearrange("p m j t -> p t m j"),
+            wu_src[0][:, :EARLY_WU_GROUPS].rearrange("p m j t -> p t m j"),
+        )
         nc.scalar.copy(wu_dst[:, EARLY_WU_GROUPS:half], wu_src[0][:, EARLY_WU_GROUPS:])
-        quantise_u(0, 1)
-        unread = psum.tile([WARM_COLUMNS, C], F32, name="unread", tag="unread")
+        unread = psum.tile([WARM_COLUMNS, C], F32, name="unread", tag="first")
         first_codes, first_plane = u_quantised[0]
         for i in range(WARM_PASSES):
             nc.tensor.matmul_mx(
@@ -157,149 +155,119 @@ def tile_moe_prv_lin_relu2_kernel(tc, uT, wu, w_words, w_scales, b, gate, offs, 
                 in_=wu_grouped[:, t * block : (t + 1) * block],
             )
 
-        weave(nc.scalar.copy, U32, 1, 2, reuse.tile([P, C * PACK], BF16, name="u_slots1", align_bytes=64, offset=0))
-        quantise_u(1, 2)
-        gather(1, 2, E)
+        woven = [
+            reuse.tile([P, C * PACK], BF16, name=f"u_slots{e}", align_bytes=64, offset=(e - 1) * 2 * C * PACK)
+            for e in range(1, E)
+        ]
+        weave(nc.scalar.copy, U32, 1, 2, woven[0])
+        weave(nc.scalar.copy, U32, 2, 3, woven[1])
+        quantise_u(1, 2, "u_codes1")
+        weave(nc.vector.tensor_copy, I32, 3, E, woven[2])
+        quantise_u(2, 3, "u_codes2")
+        quantise_u(3, E, "u_codes3")
 
         x_quantised = {}
-        y_sums = {}
         outs = {}
 
-        def project(e0, e1, banks):
-            x_grouped = keep.tile(
-                [P, (e1 - e0) * C * PACK], BF16, name=f"x_grouped{e0}", tag=f"x_grouped{e0}", align_bytes=64
-            )
-            for e in range(e0, e1):
-                u_codes, u_plane = u_quantised[e]
-                slots = x_grouped[:, (e - e0) * C * PACK : (e - e0 + 1) * C * PACK].rearrange("p (s t) -> p s t", t=PACK)
-                width = PACK // len(banks[e - e0])
-                for i, bank in enumerate(banks[e - e0]):
-                    x_sums = psum.tile([P, width, C], F32, name=f"x_sums{e}{i}", tag=bank)
-                    for t in range(i * width, (i + 1) * width):
-                        nc.tensor.matmul_mx(
-                            out=x_sums[:, t - i * width, :],
-                            lhsT=wu_codes[:, t * P : (t + 1) * P].bitcast(FP8X4),
-                            lhsT_scale=wu_plane[:, t * P : (t + 1) * P],
-                            rhs=u_codes.bitcast(FP8X4),
-                            rhs_scale=u_plane,
-                            start=True,
-                            stop=True,
-                        )
-                    nc.scalar.copy(slots[:, :, i * width : (i + 1) * width], x_sums[:].rearrange("p t s -> p s t"))
+        def project(e, banks, copy=nc.scalar.copy):
+            x_grouped = keep.tile([P, C * PACK], BF16, name=f"x_grouped{e}", align_bytes=64)
+            u_codes, u_plane = u_quantised[e]
+            slots = x_grouped[:].rearrange("p (s t) -> p s t", t=PACK)
+            width = PACK // len(banks)
+            for i, bank in enumerate(banks):
+                x_sums = psum.tile([P, width, C], F32, name=f"x_sums{e}{i}", tag=bank)
+                for t in range(i * width, (i + 1) * width):
+                    nc.tensor.matmul_mx(
+                        out=x_sums[:, t - i * width, :],
+                        lhsT=wu_codes[:, t * P : (t + 1) * P].bitcast(FP8X4),
+                        lhsT_scale=wu_plane[:, t * P : (t + 1) * P],
+                        rhs=u_codes.bitcast(FP8X4),
+                        rhs_scale=u_plane,
+                        start=True,
+                        stop=True,
+                    )
+                copy(slots[:, :, i * width : (i + 1) * width], x_sums[:].rearrange("p t s -> p s t"))
             return x_grouped
 
-        def quantise_x(e0, e1, x_grouped, x_plane):
-            x_codes = keep.tile([P, (e1 - e0) * C], U32, name=f"x_codes{e0}", align_bytes=64)
+        def quantise_x(e, x_grouped, x_plane=None):
+            x_codes = keep.tile([P, C], U32, name=f"x_codes{e}", align_bytes=64)
+            if x_plane is None:
+                x_plane = keep.tile([P, C], U8, name=f"x_plane{e}", align_bytes=64)[:]
             nc.vector.quantize_mx(out=x_codes[:].bitcast(FP8X4), scales=x_plane, in_=x_grouped[:])
-            for e in range(e0, e1):
-                cols = slice((e - e0) * C, (e - e0 + 1) * C)
-                x_quantised[e] = (x_codes[:, cols], x_plane[:, cols])
+            x_quantised[e] = (x_codes[:], x_plane)
 
-        def expert_matmul(sums, e, c):
+        def multiply(e, c0, c1, bank):
             x_codes, x_plane = x_quantised[e]
-            col = e * N + c * P
-            nc.tensor.matmul_mx(
-                out=sums,
-                lhsT=w_codes[:, 2 * col : 2 * (col + P)].bitcast(FP4X4),
-                lhsT_scale=w_plane[:, col : col + P],
-                rhs=x_codes.bitcast(FP8X4),
-                rhs_scale=x_plane,
-                start=True,
-                stop=True,
-            )
-
-        def multiply(e0, e1, c, bank):
-            sums = psum.tile([P, (e1 - e0) * C], F32, name=f"y_sums{e0}{c}", tag=bank)
-            for e in range(e0, e1):
-                y_sums[e, c] = sums[:, (e - e0) * C : (e - e0 + 1) * C]
-                expert_matmul(y_sums[e, c], e, c)
-
-        def rectify(e0, e1, c, tag):
-            relu = keep.tile([P, (e1 - e0) * C], F32, name=f"relu{e0}{c}", tag=tag, align_bytes=64)
-            for e in range(e0, e1):
-                nc.scalar.activation(
-                    relu[:, (e - e0) * C : (e - e0 + 1) * C], y_sums[e, c], ACT.Relu, bias=bias[:, c, e : e + 1]
+            sums = psum.tile([P, c1 - c0, C], F32, name=f"y_sums{e}{c0}{bank}", tag=bank)
+            for c in range(c0, c1):
+                col = e * N + c * P
+                nc.tensor.matmul_mx(
+                    out=sums[:, c - c0, :],
+                    lhsT=w_codes[:, 2 * col : 2 * (col + P)].bitcast(FP4X4),
+                    lhsT_scale=w_plane[:, col : col + P],
+                    rhs=x_codes.bitcast(FP8X4),
+                    rhs_scale=x_plane,
+                    start=True,
+                    stop=True,
                 )
-            return relu
+            return sums
 
-        def epilogue(e0, e1, c, relu_tag=None):
-            relu = rectify(e0, e1, c, relu_tag or f"relu{e0}{c}")
-            squared = keep.tile([P, (e1 - e0) * C], F32, name=f"squared{e0}{c}", align_bytes=64)
-            nc.scalar.activation(squared[:], relu[:], ACT.Square)
-            return squared[:], gates(e0, e1)
+        squared = keep.tile([P, CHUNKS, T], F32, name="squared", align_bytes=64)
+
+        def epilogue(e, c0, c1, bank, last_bank=None):
+            relu = keep.tile([P, c1 - c0, C], F32, name=f"relu{e}", align_bytes=64)
+            cut = c1 - 1 if last_bank else c1
+            for ca, cb, tag in ((c0, cut, bank), (cut, c1, last_bank)):
+                if ca < cb:
+                    sums = multiply(e, ca, cb, tag)
+                    for c in range(ca, cb):
+                        nc.scalar.activation(relu[:, c - c0, :], sums[:, c - ca, :], ACT.Relu, bias=bias[:, c, e : e + 1])
+            nc.scalar.activation(squared[:, c0:c1, e * C : (e + 1) * C], relu[:], ACT.Square)
 
         def window(c, s0, s1):
             if c not in outs:
-                tag = "x_grouped2" if c == CHUNKS - 1 else f"out{c}"
-                outs[c] = keep.tile([P, T], F32, name=f"out{c}", tag=tag, align_bytes=64)
-            return outs[c][:].indirect(offsets[:, s0 // 16 : s1 // 16])
+                outs[c] = keep.tile([P, T], F32, name=f"out{c}", align_bytes=64)
+            return outs[c][:].indirect(slot_offsets(s0, s1))
 
-        def scatter_product(c, s0, s1, factor, other):
-            nc.vector.tensor_tensor(window(c, s0, s1), factor, other, ALU.mult)
+        def scatter_gated(c, s0, s1):
+            nc.vector.tensor_tensor(window(c, s0, s1), squared[:, c, s0:s1], gate_rows[:, s0:s1], ALU.mult)
 
-        def scatter_copy(c, s0, s1, product):
-            nc.scalar.activation(window(c, s0, s1), product, ACT.Copy)
+        def product(c, s0, s1):
+            gated = keep.tile([P, s1 - s0], F32, name=f"product{c}", align_bytes=64)
+            nc.vector.tensor_tensor(gated[:], squared[:, c, s0:s1], gate_rows[:, s0:s1], ALU.mult)
+            return gated
 
-        x_first = project(0, 1, [("x0_low", "x0_high")])
-        quantise_x(0, 1, x_first, keep.tile([P, C], U8, name="x_plane0", align_bytes=64)[:])
-        x_second = project(1, 2, [("x1",)])
-        weave(
-            nc.vector.tensor_copy,
-            I32,
-            2,
-            E,
-            keep.tile([P, 2 * C * PACK], BF16, name="u_slots2", tag="u_codes1", align_bytes=64),
-        )
-        quantise_u(2, E)
+        x0 = project(0, ("x0_low", "x0_high"))
+        quantise_x(0, x0)
+        x1 = project(1, ("x1",))
+        x2 = project(2, ("x2",), nc.vector.tensor_copy)
+        x3 = project(3, ("x3",))
+        quantise_x(1, x1)
+        quantise_x(2, x2)
 
-        multiply(0, 1, 0, "first")
-        twin = psum.tile([P, C], F32, name="y_twin", tag="twin")
-        expert_matmul(twin[:], 0, 0)
-        gated = keep.tile([P, C], F32, name="gated")
-        nc.vector.scalar_tensor_tensor(gated[:], twin[:], bias[:, 0, 0:1], gates(0, 1), ALU.add, ALU.mult)
-        quantise_x(1, 2, x_second, w_codes[:, :C])
-        multiply(0, 1, 1, "y01")
-        multiply(0, 1, 2, "y02")
-        scatter_product(0, 0, C, gated[:], rectify(0, 1, 0, "relu00")[:])
-        scatter_product(1, 0, C, *epilogue(0, 1, 1, relu_tag="x_grouped2"))
-        last_of_first = epilogue(0, 1, 2)
+        first = multiply(0, 0, 1, "first")
+        first_relu = keep.tile([P, C], F32, name="first_relu")
+        first_gated = keep.tile([P, C], F32, name="first_gated")
+        nc.scalar.activation(first_relu[:], first[:, 0, :], ACT.Relu, bias=bias[:, 0, 0:1])
+        twin = multiply(0, 0, 1, "twin")
+        nc.vector.scalar_tensor_tensor(first_gated[:], twin[:, 0, :], bias[:, 0, 0:1], gate_rows[:, :C], ALU.add, ALU.mult)
+        epilogue(0, 1, CHUNKS, "y0")
+        quantise_x(3, x3, w_codes[:, 2 * P : 2 * P + C])
+        nc.vector.tensor_tensor(window(0, 0, C), first_relu[:], first_gated[:], ALU.mult)
+        scatter_gated(1, 0, C)
 
-        x_late = project(2, E, [("first",), ("twin",)])
-        quantise_x(2, E, x_late, keep.tile([P, 2 * C], U8, name="x_plane2", align_bytes=64)[:])
-        scatter_product(2, 0, C, *last_of_first)
-        multiply(1, 2, 0, "twin")
-        scatter_product(0, C, 2 * C, *epilogue(1, 2, 0))
-
-        handover = T - LAST_CHUNK_SLOTS
-        products = keep.tile([P, handover], F32, name="products", tag="u_codes2", align_bytes=64)
-
-        pair_sums = psum.tile([P, 2, C], F32, name="pair_sums", tag="first")
-        pair_relu = keep.tile([P, 2, C], F32, name="pair_relu", align_bytes=64)
-        pair_squared = keep.tile([P, 2, C], F32, name="pair_squared", align_bytes=64)
-        for c in (1, 2):
-            expert_matmul(pair_sums[:, c - 1, :], 1, c)
-        for c in (1, 2):
-            nc.scalar.activation(pair_relu[:, c - 1, :], pair_sums[:, c - 1, :], ACT.Relu, bias=bias[:, c, 1:2])
-        nc.scalar.activation(pair_squared[:], pair_relu[:], ACT.Square)
-        nc.vector.tensor_tensor(
-            products[:, : 2 * C].rearrange("p (c s) -> p c s", c=2),
-            pair_squared[:],
-            gates(1, 2).unsqueeze(1).to_broadcast([P, 2, C]),
-            ALU.mult,
-        )
-
-        multiply(2, E, 2, "x0_high")
-        squared, gate_late = epilogue(2, E, 2)
-        kept = handover - 2 * C
-        nc.vector.tensor_tensor(products[:, 2 * C :], squared[:, :kept], gate_late[:, :kept], ALU.mult)
-        scatter_product(2, handover, T, squared[:, kept:], gate_late[:, kept:])
-        multiply(2, E, 0, "x0_low")
-        scatter_product(0, 2 * C, T, *epilogue(2, E, 0))
-        multiply(2, E, 1, "x1")
-        middle_of_late = epilogue(2, E, 1)
-        scatter_copy(1, C, 2 * C, products[:, :C])
-        scatter_product(1, 2 * C, T, *middle_of_late)
-        scatter_copy(2, C, handover, products[:, C:])
+        handover = C + LAST_CHUNK_SLOTS
+        epilogue(1, 0, CHUNKS, "x0_low")
+        scatter_gated(2, 0, handover)
+        middle = product(1, C, 2 * C)
+        scatter_gated(0, C, 2 * C)
+        epilogue(2, 0, CHUNKS, "x0_high")
+        epilogue(3, 0, CHUNKS, "x1")
+        last = product(2, handover, T)
+        nc.scalar.activation(window(1, C, 2 * C), middle[:], ACT.Copy)
+        scatter_gated(0, 2 * C, T)
+        nc.scalar.activation(window(2, handover, T), last[:], ACT.Copy)
+        scatter_gated(1, 2 * C, T)
 
         for c in (0, 2, 1):
             nc.sync.dma_start(out[c * P : (c + 1) * P, :], outs[c][:])

@@ -24,7 +24,7 @@ EARLY_WU_GROUPS = 16
 LATE_WU_GROUPS = 40
 WARM_PASSES = 6
 WARM_COLUMNS = 32
-LAST_CHUNK_SLOTS = 64
+LAST_CHUNK_SLOTS = 32
 
 
 def tile_moe_prv_lin_relu2_kernel(tc, uT, wu, w_words, w_scales, b, gate, offs, out):
@@ -196,33 +196,35 @@ def tile_moe_prv_lin_relu2_kernel(tc, uT, wu, w_words, w_scales, b, gate, offs, 
             nc.vector.quantize_mx(out=x_codes[:].bitcast(FP8X4), scales=x_plane, in_=x_grouped[:])
             x_quantised[e] = (x_codes[:], x_plane)
 
-        def multiply(e, c0, c1, bank):
-            x_codes, x_plane = x_quantised[e]
-            sums = psum.tile([P, c1 - c0, C], F32, name=f"y_sums{e}{c0}{bank}", tag=bank)
+        def multiply(e0, e1, c0, c1, bank):
+            sums = psum.tile([P, c1 - c0, (e1 - e0) * C], F32, name=f"y_sums{e0}{c0}", tag=bank)
             for c in range(c0, c1):
-                col = e * N + c * P
-                nc.tensor.matmul_mx(
-                    out=sums[:, c - c0, :],
-                    lhsT=w_codes[:, 2 * col : 2 * (col + P)].bitcast(FP4X4),
-                    lhsT_scale=w_plane[:, col : col + P],
-                    rhs=x_codes.bitcast(FP8X4),
-                    rhs_scale=x_plane,
-                    start=True,
-                    stop=True,
-                )
+                for e in range(e0, e1):
+                    x_codes, x_plane = x_quantised[e]
+                    col = e * N + c * P
+                    nc.tensor.matmul_mx(
+                        out=sums[:, c - c0, (e - e0) * C : (e - e0 + 1) * C],
+                        lhsT=w_codes[:, 2 * col : 2 * (col + P)].bitcast(FP4X4),
+                        lhsT_scale=w_plane[:, col : col + P],
+                        rhs=x_codes.bitcast(FP8X4),
+                        rhs_scale=x_plane,
+                        start=True,
+                        stop=True,
+                    )
             return sums
 
         squared = keep.tile([P, CHUNKS, T], F32, name="squared", align_bytes=64)
 
-        def epilogue(e, c0, c1, bank, last_bank=None):
-            relu = keep.tile([P, c1 - c0, C], F32, name=f"relu{e}", align_bytes=64)
-            cut = c1 - 1 if last_bank else c1
-            for ca, cb, tag in ((c0, cut, bank), (cut, c1, last_bank)):
-                if ca < cb:
-                    sums = multiply(e, ca, cb, tag)
-                    for c in range(ca, cb):
-                        nc.scalar.activation(relu[:, c - c0, :], sums[:, c - ca, :], ACT.Relu, bias=bias[:, c, e : e + 1])
-            nc.scalar.activation(squared[:, c0:c1, e * C : (e + 1) * C], relu[:], ACT.Square)
+        def epilogue(e0, e1, c0, c1, bank):
+            sums = multiply(e0, e1, c0, c1, bank)
+            relu = keep.tile([P, c1 - c0, (e1 - e0) * C], F32, name=f"relu{e0}{c0}", align_bytes=64)
+            for c in range(c0, c1):
+                for e in range(e0, e1):
+                    cols = slice((e - e0) * C, (e - e0 + 1) * C)
+                    nc.scalar.activation(
+                        relu[:, c - c0, cols], sums[:, c - c0, cols], ACT.Relu, bias=bias[:, c, e : e + 1]
+                    )
+            nc.scalar.activation(squared[:, c0:c1, e0 * C : e1 * C], relu[:], ACT.Square)
 
         def window(c, s0, s1):
             if c not in outs:
@@ -245,29 +247,28 @@ def tile_moe_prv_lin_relu2_kernel(tc, uT, wu, w_words, w_scales, b, gate, offs, 
         quantise_x(1, x1)
         quantise_x(2, x2)
 
-        first = multiply(0, 0, 1, "first")
+        first = multiply(0, 1, 0, 1, "first")
         first_relu = keep.tile([P, C], F32, name="first_relu")
         first_gated = keep.tile([P, C], F32, name="first_gated")
-        nc.scalar.activation(first_relu[:], first[:, 0, :], ACT.Relu, bias=bias[:, 0, 0:1])
-        twin = multiply(0, 0, 1, "twin")
-        nc.vector.scalar_tensor_tensor(first_gated[:], twin[:, 0, :], bias[:, 0, 0:1], gate_rows[:, :C], ALU.add, ALU.mult)
-        epilogue(0, 1, CHUNKS, "y0")
+        nc.vector.tensor_scalar(first_relu[:], first[:, 0, :], bias[:, 0, 0:1], 0.0, ALU.add, ALU.max)
+        nc.vector.scalar_tensor_tensor(first_gated[:], first[:, 0, :], bias[:, 0, 0:1], gate_rows[:, :C], ALU.add, ALU.mult)
+        epilogue(0, 1, 1, CHUNKS, "y0")
         quantise_x(3, x3, w_codes[:, 2 * P : 2 * P + C])
         nc.vector.tensor_tensor(window(0, 0, C), first_relu[:], first_gated[:], ALU.mult)
         scatter_gated(1, 0, C)
 
         handover = C + LAST_CHUNK_SLOTS
-        epilogue(1, 0, CHUNKS, "x0_low")
-        scatter_gated(2, 0, handover)
+        epilogue(1, 2, 1, CHUNKS, "x0_low")
         middle = product(1, C, 2 * C)
-        scatter_gated(0, C, 2 * C)
-        epilogue(2, 0, CHUNKS, "x0_high")
-        epilogue(3, 0, CHUNKS, "x1")
+        scatter_gated(2, 0, handover)
+        epilogue(2, E, 1, CHUNKS, "x0_high")
         last = product(2, handover, T)
+        epilogue(1, E, 0, 1, "x1")
         nc.scalar.activation(window(1, C, 2 * C), middle[:], ACT.Copy)
-        scatter_gated(0, 2 * C, T)
+        scatter_gated(0, C, 3 * C)
+        scatter_gated(0, 3 * C, T)
         nc.scalar.activation(window(2, handover, T), last[:], ACT.Copy)
         scatter_gated(1, 2 * C, T)
 
-        for c in (0, 2, 1):
-            nc.sync.dma_start(out[c * P : (c + 1) * P, :], outs[c][:])
+        for c, queue in ((0, nc.sync), (2, nc.scalar), (1, nc.sync)):
+            queue.dma_start(out[c * P : (c + 1) * P, :], outs[c][:])

from contextlib import ExitStack

import concourse.mybir as mybir

F32 = mybir.dt.float32
BF16 = mybir.dt.bfloat16
U32 = mybir.dt.uint32
I32 = mybir.dt.int32
U16 = mybir.dt.uint16
U8 = mybir.dt.uint8
FP8X4 = mybir.dt.float8_e4m3fn_x4
FP4X4 = mybir.dt.float4_e2m1fn_x4
ACT = mybir.ActivationFunctionType
ALU = mybir.AluOpType

P = 128
PACK = 4
M, K, T, E, C, N = 512, 512, 512, 4, 128, 384
CHUNKS = N // P
FLOPS = 2 * M * K * T + 2 * K * N * T

FIRST_PAIR_TOKENS = 336
EARLY_WU_GROUPS = 16
LATE_WU_GROUPS = 40
WARM_PASSES = 6
WARM_COLUMNS = 32
LAST_CHUNK_SLOTS = 32


def tile_moe_prv_lin_relu2_kernel(tc, uT, wu, w_words, w_scales, b, gate, offs, out):
    nc = tc.nc
    with ExitStack() as ctx:
        keep = ctx.enter_context(tc.tile_pool(name="keep", bufs=1))
        psum = ctx.enter_context(tc.psum_pool(name="psum", bufs=1))

        offsets = keep.tile([P, E * C // 16], U16, name="offsets")

        block = P * PACK
        later = T - C
        wu_start = 4 * later
        stage = keep.tile([P, wu_start + PACK * block], BF16, name="stage", align_bytes=64)
        wu_grouped = stage[:, wu_start:]

        u_rows = uT.rearrange("(p j) t -> p j t", j=PACK)
        u_first = keep.tile([P, 2, T], F32, name="u_first", tag="u_first", align_bytes=64)
        u_raw = [u_first[:], wu_grouped.bitcast(F32).rearrange("p (j t) -> p j t", j=2)]
        wu_rows = wu.rearrange("(p j) k -> p j k", j=PACK)
        reuse = ctx.enter_context(tc.tile_pool(name="reuse", bufs=1))
        wu_raw = [
            keep.tile([P, PACK, K // 2], F32, name="wu_raw0", align_bytes=64),
            reuse.tile([P, PACK, K // 2], F32, name="wu_raw1", align_bytes=64, offset=0),
        ]
        nc.sync.dma_start(u_raw[0], u_rows[:, 0:2, :])
        nc.sync.dma_start(offsets[:], offs)
        for tokens in (slice(0, T // 2), slice(T // 2, T)):
            nc.sync.dma_start(u_raw[1][:, :, tokens], u_rows[:, 2:4, tokens])
        for h in range(2):
            nc.sync.dma_start(wu_raw[h][:], wu_rows[:, :, h * (K // 2) : (h + 1) * (K // 2)])

        bias = keep.tile([P, CHUNKS, E], F32, name="bias")
        nc.sync.dma_start(bias[:], b.rearrange("(c p) e -> p c e", p=P))
        gate_rows = keep.tile([P, T], F32, name="gate_rows", align_bytes=64)
        nc.sync.dma_start(gate_rows[:], gate[:P, :])

        w_plane = keep.tile([P, E * N], U8, name="w_plane", align_bytes=64)
        nc.vector.memset(w_plane[:].bitcast(I32), 0)
        for quadrant in range(4):
            nc.sync.dma_start(
                w_plane[32 * quadrant : 32 * quadrant + 4, :].bitcast(I32).rearrange("r (e n) -> r e n", e=E),
                w_scales[:, 0, 4 * quadrant : 4 * quadrant + 4, :].bitcast(I32).rearrange("e r n -> r e n"),
            )
        w_codes = keep.tile([P, E * 2 * N], U8, name="w_codes", align_bytes=64)
        nc.sync.dma_start(
            w_codes[:].bitcast(I32).rearrange("p (e n) -> p e n", e=E),
            w_words[:, 0, :, :].bitcast(I32).rearrange("e p n -> p e n"),
        )

        def slot_offsets(s0, s1):
            return offsets[:, s0 // 16 : s1 // 16]

        u_pairs = [
            keep.tile([P, T * 2], BF16, name="u_pairs0", align_bytes=64),
            keep.tile([P, T * 2], BF16, name="u_pairs1", tag="u_first", align_bytes=64),
        ]

        def cast_u(h, copy, tokens):
            dst = u_pairs[h][:].rearrange("p (t j) -> p t j", j=2)
            src = u_raw[h].rearrange("p j t -> p t j")
            for engine_copy, t0, t1 in zip(copy, tokens, tokens[1:]):
                engine_copy(dst[:, t0:t1], src[:, t0:t1])

        u_slots = {0: keep.tile([P, C * PACK], BF16, name="u_slots0", align_bytes=64)}

        def gather_first(h):
            words = u_slots[0][:].bitcast(U32).rearrange("p (s h) -> p s h", h=2)
            nc.vector.tensor_copy(words[:, :, h], u_pairs[h][:].bitcast(U32).indirect(slot_offsets(0, C)))

        def gather(h, e0, e1):
            row = stage[:, 2 * (h * later + (e0 - 1) * C) : 2 * (h * later + (e1 - 1) * C)]
            nc.vector.tensor_copy(row.bitcast(U32), u_pairs[h][:].bitcast(U32).indirect(slot_offsets(e0 * C, e1 * C)))

        def weave(copy, dtype, e0, e1, woven):
            u_slots[e0] = woven
            rows = stage[:, : 4 * later].bitcast(dtype).rearrange("p (h s) -> p s h", h=2)
            copy(woven[:].bitcast(dtype).rearrange("p (s h) -> p s h", h=2), rows[:, (e0 - 1) * C : (e1 - 1) * C, :])

        u_quantised = {}

        def quantise_u(e0, e1, tag):
            u_codes = keep.tile([P, (e1 - e0) * C], U32, name=f"u_codes{e0}", tag=tag, align_bytes=64)
            u_plane = keep.tile([P, (e1 - e0) * C], U8, name=f"u_plane{e0}", align_bytes=64)
            nc.vector.quantize_mx(out=u_codes[:].bitcast(FP8X4), scales=u_plane[:], in_=u_slots[e0][:])
            for e in range(e0, e1):
                cols = slice((e - e0) * C, (e - e0 + 1) * C)
                u_quantised[e] = (u_codes[:, cols], u_plane[:, cols])

        cast_u(0, (nc.vector.tensor_copy, nc.scalar.copy), (0, FIRST_PAIR_TOKENS, T))
        gather_first(0)
        gather(0, 1, E)
        cast_u(1, (nc.scalar.copy, nc.scalar.copy, nc.gpsimd.tensor_copy), (0, T // 2, 3 * T // 4, T))
        gather_first(1)
        gather(1, 1, E)
        quantise_u(0, 1, "u_codes0")

        half = P // 2
        split = half + LATE_WU_GROUPS
        wu_dst = wu_grouped.rearrange("p (t m j) -> p m j t", t=PACK, j=PACK)
        wu_src = [wu_raw[h][:].rearrange("p j (m t) -> p m j t", t=PACK) for h in range(2)]
        nc.gpsimd.tensor_copy(
            wu_dst[:, :EARLY_WU_GROUPS].rearrange("p m j t -> p t m j"),
            wu_src[0][:, :EARLY_WU_GROUPS].rearrange("p m j t -> p t m j"),
        )
        nc.scalar.copy(wu_dst[:, EARLY_WU_GROUPS:half], wu_src[0][:, EARLY_WU_GROUPS:])
        unread = psum.tile([WARM_COLUMNS, C], F32, name="unread", tag="first")
        first_codes, first_plane = u_quantised[0]
        for i in range(WARM_PASSES):
            nc.tensor.matmul_mx(
                out=unread[:],
                lhsT=first_codes[:, :WARM_COLUMNS].bitcast(FP8X4),
                lhsT_scale=first_plane[:, :WARM_COLUMNS],
                rhs=first_codes.bitcast(FP8X4),
                rhs_scale=first_plane,
                start=True,
                stop=True,
            )
        for t in range(0, PACK, 2):
            nc.vector.tensor_copy(wu_dst[:, half:split, :, t : t + 2], wu_src[1][:, :LATE_WU_GROUPS, :, t : t + 2])
            nc.scalar.copy(wu_dst[:, split:, :, t : t + 2], wu_src[1][:, LATE_WU_GROUPS:, :, t : t + 2])
        wu_codes = keep.tile([P, K], U32, name="wu_codes", align_bytes=64)
        wu_plane = keep.tile([P, K], U8, name="wu_plane", align_bytes=64)
        for t in range(PACK):
            nc.vector.quantize_mx(
                out=wu_codes[:, t * P : (t + 1) * P].bitcast(FP8X4),
                scales=wu_plane[:, t * P : (t + 1) * P],
                in_=wu_grouped[:, t * block : (t + 1) * block],
            )

        woven = [
            reuse.tile([P, C * PACK], BF16, name=f"u_slots{e}", align_bytes=64, offset=(e - 1) * 2 * C * PACK)
            for e in range(1, E)
        ]
        weave(nc.scalar.copy, U32, 1, 2, woven[0])
        weave(nc.scalar.copy, U32, 2, 3, woven[1])
        quantise_u(1, 2, "u_codes1")
        weave(nc.vector.tensor_copy, I32, 3, E, woven[2])
        quantise_u(2, 3, "u_codes2")
        quantise_u(3, E, "u_codes3")

        x_quantised = {}
        outs = {}

        def project(e, banks, copy=nc.scalar.copy):
            x_grouped = keep.tile([P, C * PACK], BF16, name=f"x_grouped{e}", align_bytes=64)
            u_codes, u_plane = u_quantised[e]
            slots = x_grouped[:].rearrange("p (s t) -> p s t", t=PACK)
            width = PACK // len(banks)
            for i, bank in enumerate(banks):
                x_sums = psum.tile([P, width, C], F32, name=f"x_sums{e}{i}", tag=bank)
                for t in range(i * width, (i + 1) * width):
                    nc.tensor.matmul_mx(
                        out=x_sums[:, t - i * width, :],
                        lhsT=wu_codes[:, t * P : (t + 1) * P].bitcast(FP8X4),
                        lhsT_scale=wu_plane[:, t * P : (t + 1) * P],
                        rhs=u_codes.bitcast(FP8X4),
                        rhs_scale=u_plane,
                        start=True,
                        stop=True,
                    )
                copy(slots[:, :, i * width : (i + 1) * width], x_sums[:].rearrange("p t s -> p s t"))
            return x_grouped

        def quantise_x(e, x_grouped, x_plane=None):
            x_codes = keep.tile([P, C], U32, name=f"x_codes{e}", align_bytes=64)
            if x_plane is None:
                x_plane = keep.tile([P, C], U8, name=f"x_plane{e}", align_bytes=64)[:]
            nc.vector.quantize_mx(out=x_codes[:].bitcast(FP8X4), scales=x_plane, in_=x_grouped[:])
            x_quantised[e] = (x_codes[:], x_plane)

        def multiply(e0, e1, c0, c1, bank):
            sums = psum.tile([P, c1 - c0, (e1 - e0) * C], F32, name=f"y_sums{e0}{c0}", tag=bank)
            for c in range(c0, c1):
                for e in range(e0, e1):
                    x_codes, x_plane = x_quantised[e]
                    col = e * N + c * P
                    nc.tensor.matmul_mx(
                        out=sums[:, c - c0, (e - e0) * C : (e - e0 + 1) * C],
                        lhsT=w_codes[:, 2 * col : 2 * (col + P)].bitcast(FP4X4),
                        lhsT_scale=w_plane[:, col : col + P],
                        rhs=x_codes.bitcast(FP8X4),
                        rhs_scale=x_plane,
                        start=True,
                        stop=True,
                    )
            return sums

        squared = keep.tile([P, CHUNKS, T], F32, name="squared", align_bytes=64)

        def epilogue(e0, e1, c0, c1, bank):
            sums = multiply(e0, e1, c0, c1, bank)
            relu = keep.tile([P, c1 - c0, (e1 - e0) * C], F32, name=f"relu{e0}{c0}", align_bytes=64)
            for c in range(c0, c1):
                for e in range(e0, e1):
                    cols = slice((e - e0) * C, (e - e0 + 1) * C)
                    nc.scalar.activation(
                        relu[:, c - c0, cols], sums[:, c - c0, cols], ACT.Relu, bias=bias[:, c, e : e + 1]
                    )
            nc.scalar.activation(squared[:, c0:c1, e0 * C : e1 * C], relu[:], ACT.Square)

        def window(c, s0, s1):
            if c not in outs:
                outs[c] = keep.tile([P, T], F32, name=f"out{c}", align_bytes=64)
            return outs[c][:].indirect(slot_offsets(s0, s1))

        def scatter_gated(c, s0, s1):
            nc.vector.tensor_tensor(window(c, s0, s1), squared[:, c, s0:s1], gate_rows[:, s0:s1], ALU.mult)

        def product(c, s0, s1):
            gated = keep.tile([P, s1 - s0], F32, name=f"product{c}", align_bytes=64)
            nc.vector.tensor_tensor(gated[:], squared[:, c, s0:s1], gate_rows[:, s0:s1], ALU.mult)
            return gated

        x0 = project(0, ("x0_low", "x0_high"))
        quantise_x(0, x0)
        x1 = project(1, ("x1",))
        x2 = project(2, ("x2",), nc.vector.tensor_copy)
        x3 = project(3, ("x3",))
        quantise_x(1, x1)
        quantise_x(2, x2)

        first = multiply(0, 1, 0, 1, "first")
        first_relu = keep.tile([P, C], F32, name="first_relu")
        first_gated = keep.tile([P, C], F32, name="first_gated")
        nc.vector.tensor_scalar(first_relu[:], first[:, 0, :], bias[:, 0, 0:1], 0.0, ALU.add, ALU.max)
        nc.vector.scalar_tensor_tensor(first_gated[:], first[:, 0, :], bias[:, 0, 0:1], gate_rows[:, :C], ALU.add, ALU.mult)
        epilogue(0, 1, 1, CHUNKS, "y0")
        quantise_x(3, x3, w_codes[:, 2 * P : 2 * P + C])
        nc.vector.tensor_tensor(window(0, 0, C), first_relu[:], first_gated[:], ALU.mult)
        scatter_gated(1, 0, C)

        handover = C + LAST_CHUNK_SLOTS
        epilogue(1, 2, 1, CHUNKS, "x0_low")
        middle = product(1, C, 2 * C)
        scatter_gated(2, 0, handover)
        epilogue(2, E, 1, CHUNKS, "x0_high")
        last = product(2, handover, T)
        epilogue(1, E, 0, 1, "x1")
        nc.scalar.activation(window(1, C, 2 * C), middle[:], ACT.Copy)
        scatter_gated(0, C, 3 * C)
        scatter_gated(0, 3 * C, T)
        nc.scalar.activation(window(2, handover, T), last[:], ACT.Copy)
        scatter_gated(1, 2 * C, T)

        for c, queue in ((0, nc.sync), (2, nc.scalar), (1, nc.sync)):
            queue.dma_start(out[c * P : (c + 1) * P, :], outs[c][:])
